import numpy as np
import ml_dtypes


def mxq(x, axis, fmt="e4m3"):
    dtype, down = {"e4m3": (ml_dtypes.float8_e4m3fn, 7), "e5m2": (ml_dtypes.float8_e5m2, 14)}[fmt]
    v = np.moveaxis(np.asarray(x, np.float32).astype(ml_dtypes.bfloat16).astype(np.float64), axis, -1)
    blocks = v.reshape(v.shape[:-1] + (-1, 32))
    amax = np.abs(blocks).max(-1, keepdims=True)
    byte = np.maximum(np.where(amax > 0, np.frexp(amax)[1] - 1 + 127, 0) - down, 1)
    scale = np.exp2(byte - 127.0)
    codes = (blocks / scale).astype(np.float32).astype(dtype).astype(np.float64)
    return np.moveaxis((codes * scale).reshape(v.shape), -1, axis)


WIDE = False


def mx_kscale(k):
    if not WIDE:
        return np.ones(k)
    levels = np.array([18, -18])
    if k % 512:
        return np.exp2(np.random.permutation(np.resize(levels, k // 32))).repeat(32)
    a = np.empty((k // 512, 16))
    for p in range(k // 512):
        a[p, :8] = np.random.permutation(np.resize(levels, 8))
        for g in range(8):
            far = levels[np.abs(levels - a[p, g]) >= 10]
            a[p, g + 8] = far[np.random.randint(len(far))]
    return np.exp2(a.ravel()).repeat(32)


def f64(x):
    return np.asarray(x).astype(np.float64)


def striped(idx):
    return np.tile(np.asarray(idx).reshape(-1, 16).T, (8, 1)).astype(np.uint16)


def unstriped(offs):
    return offs[:16].T.reshape(-1).astype(np.int64)


B, N, T, D, DV = 1, 1024, 2048, 512, 1024


def setup_inputs():
    n = np.random.standard_normal
    idx = np.random.permutation(T)[:B * N]
    u = np.ones(T)
    u[idx] = mx_kscale(B * N)
    coarse = lambda x: x.astype(np.float32).astype(ml_dtypes.bfloat16).astype(np.float64)
    r = np.random.randint(8, 33, T) / 16.0 * u
    return {
        "xT": (n((D, T)) / np.sqrt(N) / u).astype(np.float32),
        "dyT": (coarse(n((DV, T)))).astype(np.float32),
        "ts": np.tile(r, (128, 1)).astype(np.float32),
        "offs": striped(idx),
    }


def reference(xT, dyT, ts, offs):
    idx = unstriped(offs)
    pick = lambda x: x[:, idx].reshape(x.shape[0], B, N).transpose(1, 0, 2)
    dz = pick(f64(ts))[:, :1, :] * pick(f64(dyT))
    gw = mxq(pick(f64(xT)), 2, "e4m3") @ mxq(dz, 2, "e5m2").transpose(0, 2, 1)
    return gw

@@ -1,0 +1,172 @@
+from contextlib import ExitStack
+
+import concourse.mybir as mybir
+from concourse.masks import make_identity
+
+N, T, D, DV = 1024, 2048, 512, 1024
+FLOPS = 2 * N * D * DV
+
+F32 = mybir.dt.float32
+BF16 = mybir.dt.bfloat16
+U32 = mybir.dt.uint32
+U16 = mybir.dt.uint16
+U8 = mybir.dt.uint8
+E4M3 = mybir.dt.float8_e4m3fn_x4
+E5M2 = mybir.dt.float8_e5m2_x4
+COPY = mybir.ActivationFunctionType.Copy
+MULT = mybir.AluOpType.mult
+
+P = 128
+ORDER = ["y0","x0","y1","y2","x1","y3","y4","x2","y5","y6","y7","x3"]
+X_ON_VECTOR = ["x3"]
+SPLIT = ["x0","x1","x2","x3"]
+NB = 0
+TS_ON_SCALAR = []
+OUT_ON_VECTOR = [[3,1]]
+ZGROUPS = [[[0,4]],[[0,2],[2,3],[3,4]]]
+
+
+def tile_attend_gex_w_kernel(tc, xT, dyT, ts, offs, out):
+    nc = tc.nc
+    with ExitStack() as ctx:
+        keep = ctx.enter_context(tc.tile_pool(name="keep", bufs=1))
+        ring = ctx.enter_context(tc.tile_pool(name="ring", bufs=4))
+        turn = ctx.enter_context(tc.psum_pool(name="turn", bufs=4))
+        sums = ctx.enter_context(tc.psum_pool(name="sums", bufs=4))
+
+        offsets = keep.tile([P, N // 16], U16, name="offsets")
+        ts_window = keep.tile([P, T], F32, name="ts_window")
+        direct = T - P * NB
+        if NB:
+            ts_small = keep.tile([P, NB], F32, name="ts_small")
+            nc.sync.dma_start(ts_small[:], ts[0:1, direct:T].rearrange("o (n m) -> (o n) m", m=NB))
+        nc.sync.dma_start(offsets[:], offs)
+        if direct:
+            nc.sync.dma_start(ts_window[:, 0:direct], ts[:, 0:direct])
+        windows = {}
+        for name in ORDER:
+            j = int(name[1])
+            source = xT if name[0] == "x" else dyT
+            windows[name] = keep.tile([P, T], F32, name="window_" + name)
+            nc.sync.dma_start(windows[name][:], source[j * P : (j + 1) * P, :])
+
+        eye_built = keep.tile([P, P], F32, name="eye_built")
+        make_identity(nc, eye_built[:])
+        eye = keep.tile([P, P], F32, name="eye")
+        nc.scalar.activation(eye[:], eye_built[:], COPY)
+
+        for k in range(NB // 4):
+            bank = turn.tile([P, 4, P], F32, name="turned")
+            for q in range(4):
+                m = 4 * k + q
+                nc.tensor.transpose(bank[:, q, :], ts_small[:, m : m + 1].to_broadcast([P, P]), eye[:])
+            target = ts_window[:, direct:T].rearrange("p (n k q) -> p k n q", k=NB // 4, q=4)[:, k]
+            if k in TS_ON_SCALAR:
+                nc.scalar.activation(target, bank[:].rearrange("p q n -> p n q"), COPY)
+            else:
+                nc.vector.tensor_copy(target, bank[:].rearrange("p q n -> p n q"))
+
+        ts_listed = keep.tile([P, N], F32, name="ts_listed")
+        nc.vector.tensor_copy(ts_listed[:], ts_window[:].indirect(offsets[:]))
+
+        z_staged = [[keep.tile([P, 512, 4], BF16, name="z_staged%d%d" % (h, g), align_bytes=64) for g in range(2)] for h in range(2)]
+        z_codes = [[keep.tile([P, 512], U32, name="z_codes%d%d" % (h, g), align_bytes=64) for g in range(2)] for h in range(2)]
+        z_scales = [[keep.tile([P, 512], U8, name="z_scales%d%d" % (h, g), align_bytes=64) for g in range(2)] for h in range(2)]
+        x_codes = [keep.tile([P, 2 * P], U32, name="x_codes%d" % j, align_bytes=64) for j in range(4)]
+        x_scales = [keep.tile([P, 2 * P], U8, name="x_scales%d" % j, align_bytes=64) for j in range(4)]
+
+        def pieces(name):
+            return [(0, 1), (1, 2)] if name in SPLIT else [(0, 2)]
+
+        def do_dy(name):
+            j = int(name[1])
+            h, c = divmod(j, 4)
+            listed = ring.tile([P, N], F32, name="dz_listed")
+            for g0, g1 in pieces(name):
+                nc.vector.tensor_tensor(
+                    listed[:, 512 * g0 : 512 * g1],
+                    windows[name][:].indirect(offsets[:, 32 * g0 : 32 * g1]),
+                    ts_listed[:, 512 * g0 : 512 * g1],
+                    MULT,
+                )
+                for g in range(g0, g1):
+                    bank = turn.tile([P, 4, P], F32, name="turned")
+                    for t in range(4):
+                        nc.tensor.transpose(bank[:, t, :], listed[:, 512 * g + t : 512 * (g + 1) : 4], eye[:])
+                    nc.scalar.copy(z_staged[h][g][:, c * P : (c + 1) * P, :], bank[:].rearrange("p t n -> p n t"))
+            for c0, c1 in ZGROUPS[h]:
+                if c1 - 1 == c:
+                    cols = slice(c0 * P, c1 * P)
+                    for g in range(2):
+                        nc.vector.quantize_mx(
+                            out=z_codes[h][g][:, cols].bitcast(E5M2),
+                            scales=z_scales[h][g][:, cols],
+                            in_=z_staged[h][g][:, cols, :].rearrange("p n t -> p (n t)"),
+                        )
+
+        def do_x(name):
+            j = int(name[1])
+            listed = ring.tile([P, N], BF16, name="x_listed", align_bytes=64)
+            words = listed[:].bitcast(F32)
+            on_vector = name in X_ON_VECTOR
+            in_list_order = listed[:].rearrange("p (u s i) -> p s u i", u=2, i=2)
+            if not on_vector:
+                rounded = ring.tile([P, T], BF16, name="x_rounded")
+                for c in range(2):
+                    half = slice(c * T // 2, (c + 1) * T // 2)
+                    nc.scalar.activation(rounded[:, half], windows[name][:, half], COPY)
+            staged = ring.tile([P, 2, P, 4], BF16, name="x_staged", align_bytes=64)
+            staged_words = staged[:].rearrange("p g d t -> p (g d t)").bitcast(F32).rearrange("p (g d u) -> p g d u", g=2, u=2)
+            for g0, g1 in pieces(name):
+                entries = offsets[:, 32 * g0 : 32 * g1]
+                if on_vector:
+                    nc.vector.tensor_copy(in_list_order[:, P * g0 : P * g1], windows[name][:].indirect(entries))
+                else:
+                    nc.scalar.activation(in_list_order[:, P * g0 : P * g1], rounded[:].indirect(entries), COPY)
+                bank = turn.tile([P, 2, 2, P], F32, name="turned")
+                for g in range(g0, g1):
+                    for u in range(2):
+                        source = words[:, 256 * u + P * g : 256 * u + P * (g + 1)]
+                        nc.tensor.transpose(bank[:, g, u, :], source, eye[:])
+                nc.scalar.copy(staged_words[:, g0:g1], bank[:, g0:g1].rearrange("p g u d -> p g d u"))
+                cols = slice(g0 * P, g1 * P)
+                nc.vector.quantize_mx(
+                    out=x_codes[j][:, cols].bitcast(E4M3),
+                    scales=x_scales[j][:, cols],
+                    in_=staged[:, g0:g1].rearrange("p g d t -> p (g d t)"),
+                )
+
+        def do_product(j, h):
+            acc = sums.tile([P, 512], F32, name="acc")
+            for g in range(2):
+                cols = slice(g * P, (g + 1) * P)
+                nc.tensor.matmul_mx(
+                    out=acc[:],
+                    lhsT=x_codes[j][:, cols].bitcast(E4M3),
+                    lhsT_scale=x_scales[j][:, cols],
+                    rhs=z_codes[h][g][:].bitcast(E5M2),
+                    rhs_scale=z_scales[h][g][:],
+                    start=(g == 0),
+                    stop=(g == 1),
+                )
+            result = keep.tile([P, 512], F32, name="result%d%d" % (j, h))
+            if [j, h] in OUT_ON_VECTOR:
+                nc.vector.tensor_copy(result[:], acc[:])
+            else:
+                nc.scalar.copy(result[:], acc[:])
+            nc.sync.dma_start(out[0, j * P : (j + 1) * P, h * 512 : (h + 1) * 512], result[:])
+
+        done = set()
+        multiplied = set()
+        for name in ORDER:
+            if name[0] == "x":
+                do_x(name)
+            else:
+                do_dy(name)
+            done.add(name)
+            for h in range(2):
+                for j in range(4):
+                    ready = "x%d" % j in done and all("y%d" % (4 * h + c) in done for c in range(4))
+                    if ready and (j, h) not in multiplied:
+                        multiplied.add((j, h))
+                        do_product(j, h)

@@ -17,156 +17,209 @@ COPY = mybir.ActivationFunctionType.Copy
 MULT = mybir.AluOpType.mult
 
 P = 128
-ORDER = ["y0","x0","y1","y2","x1","y3","y4","x2","y5","y6","y7","x3"]
-X_ON_VECTOR = ["x3"]
-SPLIT = ["x0","x1","x2","x3"]
-NB = 0
-TS_ON_SCALAR = []
-OUT_ON_VECTOR = [[3,1]]
-ZGROUPS = [[[0,4]],[[0,2],[2,3],[3,4]]]
+NB = 16
+SPLIT = ["x0","x1","x2","x3","y7"]
+X_GATHER = {"x0":"SS","x1":"SS","x2":"SS","x3":"VV"}
+CAST_ON_VECTOR = []
+TS_ON_SCALAR = [0,2]
+OUT_ON_VECTOR = [[1,1],[3,1]]
+ZGROUPS = [[[0,4]],[[0,4]]]
+NCAST = {"x0":1,"x1":1,"x2":1}
+TEXT = ["Lsm","Loff","Lx0","Ly0","Lx1","Ly1","Ly2","Ly3","Ly4","Lx2","Ly5","Ly6","Ly7","Lx3","eye","tsT0","tsE0","tsT1","tsE1","tsT2","tsE2","tsT3","tsE3","tsg","x0c0","x0g0","x0T0","x0g1","x0T1","x0E0","x0E1","x1c0","y0g0","y0T0","y0T1","y0E0","y0E1","x0q0","x0q1","x1g0","x1T0","x1g1","x1T1","x1E0","x1E1","y1g0","y1T0","y1T1","y1E0","y1E1","y2g0","y2T0","y2T1","y2E0","y2E1","y3g0","y3T0","y3T1","y3E0","y3E1","x2c0","y4g0","y4T0","y4T1","y4E0","y4E1","zq000","zq010","x1q0","x1q1","mm00a","mm00b","mm10a","mm10b","x2g0","x2T0","x2g1","x2T1","x2E0","x2E1","y5g0","y5T0","y5T1","y5E0","y5E1","y6g0","y6T0","y6T1","y6E0","y6E1","y7g0","y7T0","y7E0","y7g1","y7T1","y7E1","x2q0","x2q1","zq100","mm20a","mm20b","oe00","st00","oe10","st10","mm01a","mm11a","mm21a","x3g0","x3T0","x3E0","x3g1","zq110","x3T1","x3q0","x3E1","x3q1","oe20","st20","mm01b","mm11b","mm21b","mm30a","mm31a","mm30b","mm31b","oe01","st01","oe11","st11","oe21","st21","oe30","st30","oe31","st31"]
+HOST = {"r0":"Wsm","r1":"r0","zs000":"Wx1","zs010":"Wx1","xc00":"Wy0","xc01":"Wy0","xc10":"Wy4","xc11":"Wy4","zc00":"Wy4","zc01":"Wy4","zs100":"Wx2","zs110":"Wx2","xc20":"Wy7","xc21":"Wy7","zc10":"Wy7","zc11":"xl30","o00":"dl71","o10":"dl70","xl30":"zs100","xl31":"zs100"}
+
+
+def tile_shapes():
+    shapes = {"Wsm": ([P, max(NB, 16)], F32, 64), "Wts": ([P, T], F32, 8192)}
+    for j in range(8):
+        shapes["Wy%d" % j] = ([P, T], F32, 8192)
+        for g0 in range(2 if "y%d" % j in SPLIT else 1):
+            width = 512 if "y%d" % j in SPLIT else 1024
+            shapes["dl%d%d" % (j, g0)] = ([P, width], F32, 4 * width)
+    for j in range(4):
+        shapes["Wx%d" % j] = ([P, T], F32, 8192)
+        if "S" in X_GATHER["x%d" % j]:
+            shapes["r%d" % j] = ([P, T], BF16, 4096)
+        for g0 in range(2 if "x%d" % j in SPLIT else 1):
+            width = 512 if "x%d" % j in SPLIT else 1024
+            shapes["xl%d%d" % (j, g0)] = ([P, width], BF16, 2 * width)
+            shapes["xs%d%d" % (j, g0)] = ([P, width], BF16, 2 * width)
+            shapes["xc%d%d" % (j, g0)] = ([P, width // 4], U32, width)
+        for h in range(2):
+            shapes["o%d%d" % (j, h)] = ([P, 512], F32, 2048)
+    for h in range(2):
+        for g in range(2):
+            shapes["zc%d%d" % (h, g)] = ([P, 512], U32, 2048)
+            for c0, c1 in ZGROUPS[h]:
+                shapes["zs%d%d%d" % (h, g, c0)] = ([P, (c1 - c0) * P, 4], BF16, 1024 * (c1 - c0))
+    return shapes
+
+
+def tile_offsets(shapes):
+    guests = {name: [g for g in shapes if HOST.get(g) == name] for name in shapes}
+
+    def region(name):
+        return max(shapes[name][2], sum(region(g) for g in guests[name]))
+
+    offsets = {}
+
+    def place(name, start):
+        offsets[name] = start
+        for g in sorted(guests[name], key=region):
+            place(g, start)
+            start += region(g)
+
+    start = 0
+    for name in shapes:
+        if name not in HOST:
+            place(name, start)
+            start += region(name)
+    return offsets
 
 
 def tile_attend_gex_w_kernel(tc, xT, dyT, ts, offs, out):
     nc = tc.nc
     with ExitStack() as ctx:
         keep = ctx.enter_context(tc.tile_pool(name="keep", bufs=1))
-        ring = ctx.enter_context(tc.tile_pool(name="ring", bufs=4))
+        arena = ctx.enter_context(tc.tile_pool(name="arena", bufs=1))
         turn = ctx.enter_context(tc.psum_pool(name="turn", bufs=4))
         sums = ctx.enter_context(tc.psum_pool(name="sums", bufs=4))
 
+        shapes = tile_shapes()
+        places = tile_offsets(shapes)
+        tiles = {}
+
+        def get(name):
+            if name not in tiles:
+                tiles[name] = arena.tile(shapes[name][0], shapes[name][1], name=name, align_bytes=64, offset=places[name])
+            return tiles[name]
+
         offsets = keep.tile([P, N // 16], U16, name="offsets")
-        ts_window = keep.tile([P, T], F32, name="ts_window")
-        direct = T - P * NB
-        if NB:
-            ts_small = keep.tile([P, NB], F32, name="ts_small")
-            nc.sync.dma_start(ts_small[:], ts[0:1, direct:T].rearrange("o (n m) -> (o n) m", m=NB))
-        nc.sync.dma_start(offsets[:], offs)
-        if direct:
-            nc.sync.dma_start(ts_window[:, 0:direct], ts[:, 0:direct])
-        windows = {}
-        for name in ORDER:
-            j = int(name[1])
-            source = xT if name[0] == "x" else dyT
-            windows[name] = keep.tile([P, T], F32, name="window_" + name)
-            nc.sync.dma_start(windows[name][:], source[j * P : (j + 1) * P, :])
-
-        eye_built = keep.tile([P, P], F32, name="eye_built")
-        make_identity(nc, eye_built[:])
         eye = keep.tile([P, P], F32, name="eye")
-        nc.scalar.activation(eye[:], eye_built[:], COPY)
-
-        for k in range(NB // 4):
-            bank = turn.tile([P, 4, P], F32, name="turned")
-            for q in range(4):
-                m = 4 * k + q
-                nc.tensor.transpose(bank[:, q, :], ts_small[:, m : m + 1].to_broadcast([P, P]), eye[:])
-            target = ts_window[:, direct:T].rearrange("p (n k q) -> p k n q", k=NB // 4, q=4)[:, k]
-            if k in TS_ON_SCALAR:
-                nc.scalar.activation(target, bank[:].rearrange("p q n -> p n q"), COPY)
-            else:
-                nc.vector.tensor_copy(target, bank[:].rearrange("p q n -> p n q"))
-
         ts_listed = keep.tile([P, N], F32, name="ts_listed")
-        nc.vector.tensor_copy(ts_listed[:], ts_window[:].indirect(offsets[:]))
-
-        z_staged = [[keep.tile([P, 512, 4], BF16, name="z_staged%d%d" % (h, g), align_bytes=64) for g in range(2)] for h in range(2)]
-        z_codes = [[keep.tile([P, 512], U32, name="z_codes%d%d" % (h, g), align_bytes=64) for g in range(2)] for h in range(2)]
         z_scales = [[keep.tile([P, 512], U8, name="z_scales%d%d" % (h, g), align_bytes=64) for g in range(2)] for h in range(2)]
-        x_codes = [keep.tile([P, 2 * P], U32, name="x_codes%d" % j, align_bytes=64) for j in range(4)]
         x_scales = [keep.tile([P, 2 * P], U8, name="x_scales%d" % j, align_bytes=64) for j in range(4)]
+        banks = {}
+        direct = T - P * NB
 
-        def pieces(name):
-            return [(0, 1), (1, 2)] if name in SPLIT else [(0, 2)]
+        def span(name, g0):
+            return g0 + 1 if name in SPLIT else 2
 
-        def do_dy(name):
-            j = int(name[1])
-            h, c = divmod(j, 4)
-            listed = ring.tile([P, N], F32, name="dz_listed")
-            for g0, g1 in pieces(name):
-                nc.vector.tensor_tensor(
-                    listed[:, 512 * g0 : 512 * g1],
-                    windows[name][:].indirect(offsets[:, 32 * g0 : 32 * g1]),
-                    ts_listed[:, 512 * g0 : 512 * g1],
-                    MULT,
-                )
-                for g in range(g0, g1):
-                    bank = turn.tile([P, 4, P], F32, name="turned")
-                    for t in range(4):
-                        nc.tensor.transpose(bank[:, t, :], listed[:, 512 * g + t : 512 * (g + 1) : 4], eye[:])
-                    nc.scalar.copy(z_staged[h][g][:, c * P : (c + 1) * P, :], bank[:].rearrange("p t n -> p n t"))
-            for c0, c1 in ZGROUPS[h]:
-                if c1 - 1 == c:
-                    cols = slice(c0 * P, c1 * P)
-                    for g in range(2):
-                        nc.vector.quantize_mx(
-                            out=z_codes[h][g][:, cols].bitcast(E5M2),
-                            scales=z_scales[h][g][:, cols],
-                            in_=z_staged[h][g][:, cols, :].rearrange("p n t -> p (n t)"),
-                        )
-
-        def do_x(name):
-            j = int(name[1])
-            listed = ring.tile([P, N], BF16, name="x_listed", align_bytes=64)
-            words = listed[:].bitcast(F32)
-            on_vector = name in X_ON_VECTOR
-            in_list_order = listed[:].rearrange("p (u s i) -> p s u i", u=2, i=2)
-            if not on_vector:
-                rounded = ring.tile([P, T], BF16, name="x_rounded")
-                for c in range(2):
-                    half = slice(c * T // 2, (c + 1) * T // 2)
-                    nc.scalar.activation(rounded[:, half], windows[name][:, half], COPY)
-            staged = ring.tile([P, 2, P, 4], BF16, name="x_staged", align_bytes=64)
-            staged_words = staged[:].rearrange("p g d t -> p (g d t)").bitcast(F32).rearrange("p (g d u) -> p g d u", g=2, u=2)
-            for g0, g1 in pieces(name):
-                entries = offsets[:, 32 * g0 : 32 * g1]
-                if on_vector:
-                    nc.vector.tensor_copy(in_list_order[:, P * g0 : P * g1], windows[name][:].indirect(entries))
+        for step in TEXT:
+            if step == "Lsm":
+                nc.sync.dma_start(get("Wsm")[:, 0:NB], ts[0:1, direct:T].rearrange("o (n m) -> (o n) m", m=NB))
+            elif step == "Loff":
+                nc.sync.dma_start(offsets[:], offs)
+            elif step == "Lts":
+                nc.sync.dma_start(get("Wts")[:, 0:direct], ts[:, 0:direct])
+            elif step[0] == "L":
+                j = int(step[2])
+                source = xT if step[1] == "x" else dyT
+                nc.sync.dma_start(get("W" + step[1:])[:], source[j * P : (j + 1) * P, :])
+            elif step == "eye":
+                make_identity(nc, eye[:])
+            elif step[:3] == "tsT":
+                k = int(step[3])
+                banks[step] = turn.tile([P, 4, P], F32, name="turned")
+                for q in range(4):
+                    m = 4 * k + q
+                    nc.tensor.transpose(banks[step][:, q, :], get("Wsm")[:, m : m + 1].to_broadcast([P, P]), eye[:])
+            elif step[:3] == "tsE":
+                k = int(step[3])
+                target = get("Wts")[:, direct:T].rearrange("p (n k q) -> p k n q", k=NB // 4, q=4)[:, k]
+                source = banks["tsT%d" % k][:].rearrange("p q n -> p n q")
+                if k in TS_ON_SCALAR:
+                    nc.scalar.activation(target, source, COPY)
                 else:
-                    nc.scalar.activation(in_list_order[:, P * g0 : P * g1], rounded[:].indirect(entries), COPY)
-                bank = turn.tile([P, 2, 2, P], F32, name="turned")
-                for g in range(g0, g1):
-                    for u in range(2):
-                        source = words[:, 256 * u + P * g : 256 * u + P * (g + 1)]
-                        nc.tensor.transpose(bank[:, g, u, :], source, eye[:])
-                nc.scalar.copy(staged_words[:, g0:g1], bank[:, g0:g1].rearrange("p g u d -> p g d u"))
-                cols = slice(g0 * P, g1 * P)
+                    nc.vector.tensor_copy(target, source)
+            elif step == "tsg":
+                nc.vector.tensor_copy(ts_listed[:], get("Wts")[:].indirect(offsets[:]))
+            elif step[0] == "y":
+                name, j, kind, g = step[:2], int(step[1]), step[2], int(step[3])
+                h, c = divmod(j, 4)
+                if kind == "g":
+                    g1 = span(name, g)
+                    nc.vector.tensor_tensor(
+                        get("dl%d%d" % (j, g))[:],
+                        get("W" + name)[:].indirect(offsets[:, 32 * g : 32 * g1]),
+                        ts_listed[:, 512 * g : 512 * g1],
+                        MULT,
+                    )
+                elif kind == "T":
+                    g0 = g if name in SPLIT else 0
+                    listed = get("dl%d%d" % (j, g0))
+                    banks[step] = turn.tile([P, 4, P], F32, name="turned")
+                    for t in range(4):
+                        first = 512 * (g - g0)
+                        nc.tensor.transpose(banks[step][:, t, :], listed[:, first + t : first + 512 : 4], eye[:])
+                else:
+                    c0 = [z[0] for z in ZGROUPS[h] if z[0] <= c < z[1]][0]
+                    staged = get("zs%d%d%d" % (h, g, c0))
+                    nc.scalar.copy(
+                        staged[:, (c - c0) * P : (c - c0 + 1) * P, :],
+                        banks[name + "T%d" % g][:].rearrange("p t n -> p n t"),
+                    )
+            elif step[:2] == "zq":
+                h, g, c0 = int(step[2]), int(step[3]), int(step[4])
+                c1 = [z[1] for z in ZGROUPS[h] if z[0] == c0][0]
+                cols = slice(c0 * P, c1 * P)
                 nc.vector.quantize_mx(
-                    out=x_codes[j][:, cols].bitcast(E4M3),
-                    scales=x_scales[j][:, cols],
-                    in_=staged[:, g0:g1].rearrange("p g d t -> p (g d t)"),
+                    out=get("zc%d%d" % (h, g))[:, cols].bitcast(E5M2),
+                    scales=z_scales[h][g][:, cols],
+                    in_=get("zs%d%d%d" % (h, g, c0))[:].rearrange("p n t -> p (n t)"),
                 )
-
-        def do_product(j, h):
-            acc = sums.tile([P, 512], F32, name="acc")
-            for g in range(2):
-                cols = slice(g * P, (g + 1) * P)
+            elif step[0] == "x":
+                name, j, kind, g = step[:2], int(step[1]), step[2], int(step[3])
+                g1 = span(name, g)
+                if kind == "c":
+                    parts = NCAST.get(name, 2)
+                    half = slice(g * T // parts, (g + 1) * T // parts)
+                    if name in CAST_ON_VECTOR:
+                        nc.vector.tensor_copy(get("r%d" % j)[:, half], get("W" + name)[:, half])
+                    else:
+                        nc.scalar.activation(get("r%d" % j)[:, half], get("W" + name)[:, half], COPY)
+                elif kind == "g":
+                    in_list_order = get("xl%d%d" % (j, g))[:].rearrange("p (u s i) -> p s u i", u=2, i=2)
+                    entries = offsets[:, 32 * g : 32 * g1]
+                    if X_GATHER[name][g] == "V":
+                        nc.vector.tensor_copy(in_list_order, get("W" + name)[:].indirect(entries))
+                    else:
+                        nc.scalar.activation(in_list_order, get("r%d" % j)[:].indirect(entries), COPY)
+                elif kind == "T":
+                    words = get("xl%d%d" % (j, g))[:].bitcast(F32).rearrange("p (u g s) -> p u g s", u=2, s=P)
+                    banks[step] = turn.tile([P, 2, 2, P], F32, name="turned")
+                    for q in range(g1 - g):
+                        for u in range(2):
+                            nc.tensor.transpose(banks[step][:, q, u, :], words[:, u, q, :], eye[:])
+                elif kind == "E":
+                    staged = get("xs%d%d" % (j, g))[:].bitcast(F32).rearrange("p (g d u) -> p g d u", d=P, u=2)
+                    nc.scalar.copy(staged, banks[name + "T%d" % g][:, 0 : g1 - g].rearrange("p g u d -> p g d u"))
+                else:
+                    nc.vector.quantize_mx(
+                        out=get("xc%d%d" % (j, g))[:].bitcast(E4M3),
+                        scales=x_scales[j][:, g * P : g1 * P],
+                        in_=get("xs%d%d" % (j, g))[:],
+                    )
+            elif step[:2] == "mm":
+                j, h, g = int(step[2]), int(step[3]), ["a", "b"].index(step[4])
+                if g == 0:
+                    banks[step[2:4]] = sums.tile([P, 512], F32, name="acc")
+                g0 = g if "x%d" % j in SPLIT else 0
                 nc.tensor.matmul_mx(
-                    out=acc[:],
-                    lhsT=x_codes[j][:, cols].bitcast(E4M3),
-                    lhsT_scale=x_scales[j][:, cols],
-                    rhs=z_codes[h][g][:].bitcast(E5M2),
+                    out=banks[step[2:4]][:],
+                    lhsT=get("xc%d%d" % (j, g0))[:, (g - g0) * P : (g - g0 + 1) * P].bitcast(E4M3),
+                    lhsT_scale=x_scales[j][:, g * P : (g + 1) * P],
+                    rhs=get("zc%d%d" % (h, g))[:].bitcast(E5M2),
                     rhs_scale=z_scales[h][g][:],
                     start=(g == 0),
                     stop=(g == 1),
                 )
-            result = keep.tile([P, 512], F32, name="result%d%d" % (j, h))
-            if [j, h] in OUT_ON_VECTOR:
-                nc.vector.tensor_copy(result[:], acc[:])
+            elif step[:2] == "oe":
+                j, h = int(step[2]), int(step[3])
+                if [j, h] in OUT_ON_VECTOR:
+                    nc.vector.tensor_copy(get("o%d%d" % (j, h))[:], banks[step[2:4]][:])
+                else:
+                    nc.scalar.copy(get("o%d%d" % (j, h))[:], banks[step[2:4]][:])
             else:
-                nc.scalar.copy(result[:], acc[:])
-            nc.sync.dma_start(out[0, j * P : (j + 1) * P, h * 512 : (h + 1) * 512], result[:])
-
-        done = set()
-        multiplied = set()
-        for name in ORDER:
-            if name[0] == "x":
-                do_x(name)
-            else:
-                do_dy(name)
-            done.add(name)
-            for h in range(2):
-                for j in range(4):
-                    ready = "x%d" % j in done and all("y%d" % (4 * h + c) in done for c in range(4))
-                    if ready and (j, h) not in multiplied:
-                        multiplied.add((j, h))
-                        do_product(j, h)
+                j, h = int(step[2]), int(step[3])
+                nc.sync.dma_start(out[0, j * P : (j + 1) * P, h * 512 : (h + 1) * 512], get("o%d%d" % (j, h))[:])

@@ -25,8 +25,9 @@ TS_ON_SCALAR = [0,2]
 OUT_ON_VECTOR = [[1,1],[3,1]]
 ZGROUPS = [[[0,4]],[[0,4]]]
 NCAST = {"x0":1,"x1":1,"x2":1}
-TEXT = ["Lsm","Loff","Lx0","Ly0","Lx1","Ly1","Ly2","Ly3","Ly4","Lx2","Ly5","Ly6","Ly7","Lx3","eye","tsT0","tsE0","tsT1","tsE1","tsT2","tsE2","tsT3","tsE3","tsg","x0c0","x0g0","x0T0","x0g1","x0T1","x0E0","x0E1","x1c0","y0g0","y0T0","y0T1","y0E0","y0E1","x0q0","x0q1","x1g0","x1T0","x1g1","x1T1","x1E0","x1E1","y1g0","y1T0","y1T1","y1E0","y1E1","y2g0","y2T0","y2T1","y2E0","y2E1","y3g0","y3T0","y3T1","y3E0","y3E1","x2c0","y4g0","y4T0","y4T1","y4E0","y4E1","zq000","zq010","x1q0","x1q1","mm00a","mm00b","mm10a","mm10b","x2g0","x2T0","x2g1","x2T1","x2E0","x2E1","y5g0","y5T0","y5T1","y5E0","y5E1","y6g0","y6T0","y6T1","y6E0","y6E1","y7g0","y7T0","y7E0","y7g1","y7T1","y7E1","x2q0","x2q1","zq100","mm20a","mm20b","oe00","st00","oe10","st10","mm01a","mm11a","mm21a","x3g0","x3T0","x3E0","x3g1","zq110","x3T1","x3q0","x3E1","x3q1","oe20","st20","mm01b","mm11b","mm21b","mm30a","mm31a","mm30b","mm31b","oe01","st01","oe11","st11","oe21","st21","oe30","st30","oe31","st31"]
-HOST = {"r0":"Wsm","r1":"r0","zs000":"Wx1","zs010":"Wx1","xc00":"Wy0","xc01":"Wy0","xc10":"Wy4","xc11":"Wy4","zc00":"Wy4","zc01":"Wy4","zs100":"Wx2","zs110":"Wx2","xc20":"Wy7","xc21":"Wy7","zc10":"Wy7","zc11":"xl30","o00":"dl71","o10":"dl70","xl30":"zs100","xl31":"zs100"}
+HALVED = [[3,0],[3,1]]
+TEXT = ["Lsm","Loff","Lx0","Ly0","Lx1","Ly1","Ly2","Ly3","Ly4","Lx2","Ly5","Ly6","Ly7","Lx3","eye","tsT0","tsE0","tsT1","tsE1","tsT2","tsE2","tsT3","tsE3","tsg","x0c0","x0g0","x0T0","x0g1","x0T1","x0E0","x1c0","x0E1","y0g0","y0T0","y0T1","y0E0","y0E1","x1g0","x1T0","y1g0","y1T0","y1T1","y1E0","y1E1","x0q0","x0q1","x1E0","x1g1","x1T1","y2g0","y2T0","y2T1","y2E0","y2E1","x1E1","y3g0","y3T0","y3T1","y3E0","y3E1","x2c0","y4g0","y4T0","y4T1","y4E0","y4E1","zq000","zq010","x1q0","x1q1","mm00a","mm00b","mm10a","mm10b","x2g0","x2T0","x2g1","x2T1","y5g0","y5T0","y5T1","y5E0","y5E1","x2E0","x2E1","y6g0","y6T0","y6T1","y6E0","y6E1","y7g0","y7T0","y7E0","y7g1","y7T1","y7E1","x2q0","x2q1","mm20a","mm20b","x3g0","x3T0","zq100","zq110","oe00","st00","oe10","st10","x3E0","mm01a","mm11a","mm21a","mm01b","mm11b","x3g1","x3T1","x3q0","x3E1","x3q1","oe20","st20","mm21b","oe01","st01","mm30a","mm31a","mm30b","mm31b","oe11","st11","oe21","st21","oe30","st30","oe31","st31"]
+HOST = {"r0":"Wsm","r1":"r0","zs000":"Wx1","zs010":"Wx1","xc00":"Wy1","xc01":"Wy1","xc10":"Wy4","xc11":"Wy4","zc00":"Wy4","zc01":"Wy4","r2":"dl30","zs100":"Wx2","zs110":"Wx2","xs20":"dl50","xs21":"dl50","xc20":"Wy7","xc21":"Wy7","xl31":"zs110","o00":"dl71","o10":"zs100","xl30":"xs21"}
 
 
 def tile_shapes():
@@ -112,10 +113,15 @@ def tile_attend_gex_w_kernel(tc, xT, dyT, ts, offs, out):
                 nc.sync.dma_start(offsets[:], offs)
             elif step == "Lts":
                 nc.sync.dma_start(get("Wts")[:, 0:direct], ts[:, 0:direct])
-            elif step[0] == "L":
+            elif step[0] in "LM":
                 j = int(step[2])
                 source = xT if step[1] == "x" else dyT
-                nc.sync.dma_start(get("W" + step[1:])[:], source[j * P : (j + 1) * P, :])
+                cols = slice(0, T)
+                if step[0] == "M":
+                    cols = slice(0, T // 2)
+                elif "M" + step[1:] in TEXT:
+                    cols = slice(T // 2, T)
+                nc.sync.dma_start(get("W" + step[1:])[:, cols], source[j * P : (j + 1) * P, cols])
             elif step == "eye":
                 make_identity(nc, eye[:])
             elif step[:3] == "tsT":
@@ -216,10 +222,17 @@ def tile_attend_gex_w_kernel(tc, xT, dyT, ts, offs, out):
                 )
             elif step[:2] == "oe":
                 j, h = int(step[2]), int(step[3])
-                if [j, h] in OUT_ON_VECTOR:
-                    nc.vector.tensor_copy(get("o%d%d" % (j, h))[:], banks[step[2:4]][:])
-                else:
-                    nc.scalar.copy(get("o%d%d" % (j, h))[:], banks[step[2:4]][:])
+                width = 256 if [j, h] in HALVED else 512
+                for c in range(0, 512, width):
+                    if [j, h] in OUT_ON_VECTOR:
+                        nc.vector.tensor_copy(get("o%d%d" % (j, h))[:, c : c + width], banks[step[2:4]][:, c : c + width])
+                    else:
+                        nc.scalar.copy(get("o%d%d" % (j, h))[:, c : c + width], banks[step[2:4]][:, c : c + width])
             else:
                 j, h = int(step[2]), int(step[3])
-                nc.sync.dma_start(out[0, j * P : (j + 1) * P, h * 512 : (h + 1) * 512], get("o%d%d" % (j, h))[:])
+                width = 256 if [j, h] in HALVED else 512
+                for c in range(0, 512, width):
+                    nc.sync.dma_start(
+                        out[0, j * P : (j + 1) * P, h * 512 + c : h * 512 + c + width],
+                        get("o%d%d" % (j, h))[:, c : c + width],
+                    )

@@ -26,8 +26,8 @@ OUT_ON_VECTOR = [[1,1],[3,1]]
 ZGROUPS = [[[0,4]],[[0,4]]]
 NCAST = {"x0":1,"x1":1,"x2":1}
 HALVED = [[3,0],[3,1]]
-TEXT = ["Lsm","Loff","Lx0","Ly0","Lx1","Ly1","Ly2","Ly3","Ly4","Lx2","Ly5","Ly6","Ly7","Lx3","eye","tsT0","tsE0","tsT1","tsE1","tsT2","tsE2","tsT3","tsE3","tsg","x0c0","x0g0","x0T0","x0g1","x0T1","x0E0","x1c0","x0E1","y0g0","y0T0","y0T1","y0E0","y0E1","x1g0","x1T0","y1g0","y1T0","y1T1","y1E0","y1E1","x0q0","x0q1","x1E0","x1g1","x1T1","y2g0","y2T0","y2T1","y2E0","y2E1","x1E1","y3g0","y3T0","y3T1","y3E0","y3E1","x2c0","y4g0","y4T0","y4T1","y4E0","y4E1","zq000","zq010","x1q0","x1q1","mm00a","mm00b","mm10a","mm10b","x2g0","x2T0","x2g1","x2T1","y5g0","y5T0","y5T1","y5E0","y5E1","x2E0","x2E1","y6g0","y6T0","y6T1","y6E0","y6E1","y7g0","y7T0","y7E0","y7g1","y7T1","y7E1","x2q0","x2q1","mm20a","mm20b","x3g0","x3T0","zq100","zq110","oe00","st00","oe10","st10","x3E0","mm01a","mm11a","mm21a","mm01b","mm11b","x3g1","x3T1","x3q0","x3E1","x3q1","oe20","st20","mm21b","oe01","st01","mm30a","mm31a","mm30b","mm31b","oe11","st11","oe21","st21","oe30","st30","oe31","st31"]
-HOST = {"r0":"Wsm","r1":"r0","zs000":"Wx1","zs010":"Wx1","xc00":"Wy1","xc01":"Wy1","xc10":"Wy4","xc11":"Wy4","zc00":"Wy4","zc01":"Wy4","r2":"dl30","zs100":"Wx2","zs110":"Wx2","xs20":"dl50","xs21":"dl50","xc20":"Wy7","xc21":"Wy7","xl31":"zs110","o00":"dl71","o10":"zs100","xl30":"xs21"}
+TEXT = ["Lsm","Loff","Lx0","Ly0","Lx1","Ly1","Ly2","Ly3","Ly4","Lx2","Ly5","Ly6","Ly7","Lx3","eye","tsT0","tsE0","tsT1","tsE1","tsT2","tsE2","tsT3","tsE3","tsg","y0g0","x0c0","x0g1","x0g0","x0T0","x0E0","x1c0","x1g0","y1g0","y0T0","y0T1","y0E0","y0E1","y3g0","x1g1","y1T0","y1T1","y1E0","y1E1","x3g1","y2g0","x0T1","x0E1","x1T0","x1E0","x1T1","x1E1","y2T0","y2T1","y2E0","y2E1","y4g0","y3T0","y3T1","y3E0","y3E1","zq000","zq010","y4T0","y4T1","y4E0","y4E1","x2c0","y7g0","x1q0","x1q1","y6g0","x2g0","x0q0","x0q1","x2g1","y6T0","y6T1","y6E0","y6E1","x3g0","y5g0","x2T0","x2E0","x2T1","x2E1","mm00a","mm00b","y7g1","y7T0","y7E0","x2q0","x2q1","y7T1","y7E1","y5T0","y5T1","y5E0","y5E1","mm20a","mm20b","x3T1","x3E1","oe00","st00","zq100","mm10a","mm10b","x3q1","x3T0","x3E0","x3q0","zq110","mm01a","mm01b","oe01","st01","mm11a","mm11b","mm21a","mm21b","oe10","st10","mm31a","mm31b","oe21","st21","oe20","st20","mm30a","mm30b","oe31","st31","oe11","st11","oe30","st30"]
+HOST = {"r0":"Wsm","r1":"Wx0","r2":"dl30","xc20":"dl60","xc21":"dl60","xl11":"r0","zc10":"dl71","xl21":"xs10","dl40":"xl10"}
 
 
 def tile_shapes():

@@ -17,65 +17,13 @@ COPY = mybir.ActivationFunctionType.Copy
 MULT = mybir.AluOpType.mult
 
 P = 128
-NB = 16
-SPLIT = ["x0","x1","x2","x3","y7"]
-X_GATHER = {"x0":"SS","x1":"SS","x2":"SS","x3":"VV"}
-CAST_ON_VECTOR = []
-TS_ON_SCALAR = [0,2]
-OUT_ON_VECTOR = [[1,1],[3,1]]
-ZGROUPS = [[[0,4]],[[0,4]]]
-NCAST = {"x0":1,"x1":1,"x2":1}
-HALVED = [[3,0],[3,1]]
-TEXT = ["Lsm","Loff","Lx0","Ly0","Lx1","Ly1","Ly2","Ly3","Ly4","Lx2","Ly5","Ly6","Ly7","Lx3","eye","tsT0","tsE0","tsT1","tsE1","tsT2","tsE2","tsT3","tsE3","tsg","y0g0","x0c0","x0g1","x0g0","x0T0","x0E0","x1c0","x1g0","y1g0","y0T0","y0T1","y0E0","y0E1","y3g0","x1g1","y1T0","y1T1","y1E0","y1E1","x3g1","y2g0","x0T1","x0E1","x1T0","x1E0","x1T1","x1E1","y2T0","y2T1","y2E0","y2E1","y4g0","y3T0","y3T1","y3E0","y3E1","zq000","zq010","y4T0","y4T1","y4E0","y4E1","x2c0","y7g0","x1q0","x1q1","y6g0","x2g0","x0q0","x0q1","x2g1","y6T0","y6T1","y6E0","y6E1","x3g0","y5g0","x2T0","x2E0","x2T1","x2E1","mm00a","mm00b","y7g1","y7T0","y7E0","x2q0","x2q1","y7T1","y7E1","y5T0","y5T1","y5E0","y5E1","mm20a","mm20b","x3T1","x3E1","oe00","st00","zq100","mm10a","mm10b","x3q1","x3T0","x3E0","x3q0","zq110","mm01a","mm01b","oe01","st01","mm11a","mm11b","mm21a","mm21b","oe10","st10","mm31a","mm31b","oe21","st21","oe20","st20","mm30a","mm30b","oe31","st31","oe11","st11","oe30","st30"]
-HOST = {"r0":"Wsm","r1":"Wx0","r2":"dl30","xc20":"dl60","xc21":"dl60","xl11":"r0","zc10":"dl71","xl21":"xs10","dl40":"xl10"}
-
-
-def tile_shapes():
-    shapes = {"Wsm": ([P, max(NB, 16)], F32, 64), "Wts": ([P, T], F32, 8192)}
-    for j in range(8):
-        shapes["Wy%d" % j] = ([P, T], F32, 8192)
-        for g0 in range(2 if "y%d" % j in SPLIT else 1):
-            width = 512 if "y%d" % j in SPLIT else 1024
-            shapes["dl%d%d" % (j, g0)] = ([P, width], F32, 4 * width)
-    for j in range(4):
-        shapes["Wx%d" % j] = ([P, T], F32, 8192)
-        if "S" in X_GATHER["x%d" % j]:
-            shapes["r%d" % j] = ([P, T], BF16, 4096)
-        for g0 in range(2 if "x%d" % j in SPLIT else 1):
-            width = 512 if "x%d" % j in SPLIT else 1024
-            shapes["xl%d%d" % (j, g0)] = ([P, width], BF16, 2 * width)
-            shapes["xs%d%d" % (j, g0)] = ([P, width], BF16, 2 * width)
-            shapes["xc%d%d" % (j, g0)] = ([P, width // 4], U32, width)
-        for h in range(2):
-            shapes["o%d%d" % (j, h)] = ([P, 512], F32, 2048)
-    for h in range(2):
-        for g in range(2):
-            shapes["zc%d%d" % (h, g)] = ([P, 512], U32, 2048)
-            for c0, c1 in ZGROUPS[h]:
-                shapes["zs%d%d%d" % (h, g, c0)] = ([P, (c1 - c0) * P, 4], BF16, 1024 * (c1 - c0))
-    return shapes
-
-
-def tile_offsets(shapes):
-    guests = {name: [g for g in shapes if HOST.get(g) == name] for name in shapes}
-
-    def region(name):
-        return max(shapes[name][2], sum(region(g) for g in guests[name]))
-
-    offsets = {}
-
-    def place(name, start):
-        offsets[name] = start
-        for g in sorted(guests[name], key=region):
-            place(g, start)
-            start += region(g)
-
-    start = 0
-    for name in shapes:
-        if name not in HOST:
-            place(name, start)
-            start += region(name)
-    return offsets
+PASS = 512
+TS_COLS = T // P
+WINDOW_BYTES = 4 * T
+ARRIVAL = ["y0","x0","y1","y2","y3","y4","x1","y5","y6","y7","x2","x3"]
+Z_GROUP = [(0, 4)] * 4 + [(0, 2)] * 2 + [(2, 4)] * 2
+HOSTS = ARRIVAL + ["ts", "rows"]
+HALVED_LOADS = ["x2"]
 
 
 def tile_attend_gex_w_kernel(tc, xT, dyT, ts, offs, out):
@@ -86,153 +34,234 @@ def tile_attend_gex_w_kernel(tc, xT, dyT, ts, offs, out):
         turn = ctx.enter_context(tc.psum_pool(name="turn", bufs=4))
         sums = ctx.enter_context(tc.psum_pool(name="sums", bufs=4))
 
-        shapes = tile_shapes()
-        places = tile_offsets(shapes)
-        tiles = {}
-
-        def get(name):
-            if name not in tiles:
-                tiles[name] = arena.tile(shapes[name][0], shapes[name][1], name=name, align_bytes=64, offset=places[name])
-            return tiles[name]
+        def tile(name, shape, dtype, host=None, at=0):
+            if host is None:
+                return keep.tile(shape, dtype, name=name, align_bytes=64)
+            return arena.tile(shape, dtype, name=name, align_bytes=64, offset=HOSTS.index(host) * WINDOW_BYTES + at)
 
         offsets = keep.tile([P, N // 16], U16, name="offsets")
-        eye = keep.tile([P, P], F32, name="eye")
-        ts_listed = keep.tile([P, N], F32, name="ts_listed")
-        z_scales = [[keep.tile([P, 512], U8, name="z_scales%d%d" % (h, g), align_bytes=64) for g in range(2)] for h in range(2)]
-        x_scales = [keep.tile([P, 2 * P], U8, name="x_scales%d" % j, align_bytes=64) for j in range(4)]
-        banks = {}
-        direct = T - P * NB
+        eye = tile("eye", [P, P], F32)
+        ts_rows = tile("ts_rows", [P, TS_COLS], F32, "rows")
+        ts_window = tile("ts_window", [P, T], F32, "ts")
+        ts_listed = tile("ts_listed", [P, N], F32)
+        window = {name: tile("window_" + name, [P, T], F32, host=name) for name in ARRIVAL}
+        z_scales = [tile("z_scales%d" % h, [P, 2 * PASS], U8) for h in range(2)]
+        x_scales = [tile("x_scales%d" % j, [P, 2 * P], U8) for j in range(4)]
+        held = {}
 
-        def span(name, g0):
-            return g0 + 1 if name in SPLIT else 2
+        nc.sync.dma_start(ts_rows[:], ts[0:1, :].rearrange("o (n m) -> (o n) m", m=TS_COLS))
+        nc.sync.dma_start(offsets[:], offs)
+        for name in ARRIVAL:
+            j = int(name[1])
+            source = xT if name[0] == "x" else dyT
+            parts = 2 if name in HALVED_LOADS else 1
+            for k in range(parts):
+                cols = slice(k * T // parts, (k + 1) * T // parts)
+                nc.sync.dma_start(window[name][:, cols], source[j * P : (j + 1) * P, cols])
+        make_identity(nc, eye[:])
 
-        for step in TEXT:
-            if step == "Lsm":
-                nc.sync.dma_start(get("Wsm")[:, 0:NB], ts[0:1, direct:T].rearrange("o (n m) -> (o n) m", m=NB))
-            elif step == "Loff":
-                nc.sync.dma_start(offsets[:], offs)
-            elif step == "Lts":
-                nc.sync.dma_start(get("Wts")[:, 0:direct], ts[:, 0:direct])
-            elif step[0] in "LM":
-                j = int(step[2])
-                source = xT if step[1] == "x" else dyT
-                cols = slice(0, T)
-                if step[0] == "M":
-                    cols = slice(0, T // 2)
-                elif "M" + step[1:] in TEXT:
-                    cols = slice(T // 2, T)
-                nc.sync.dma_start(get("W" + step[1:])[:, cols], source[j * P : (j + 1) * P, cols])
-            elif step == "eye":
-                make_identity(nc, eye[:])
-            elif step[:3] == "tsT":
-                k = int(step[3])
-                banks[step] = turn.tile([P, 4, P], F32, name="turned")
-                for q in range(4):
-                    m = 4 * k + q
-                    nc.tensor.transpose(banks[step][:, q, :], get("Wsm")[:, m : m + 1].to_broadcast([P, P]), eye[:])
-            elif step[:3] == "tsE":
-                k = int(step[3])
-                target = get("Wts")[:, direct:T].rearrange("p (n k q) -> p k n q", k=NB // 4, q=4)[:, k]
-                source = banks["tsT%d" % k][:].rearrange("p q n -> p n q")
-                if k in TS_ON_SCALAR:
-                    nc.scalar.activation(target, source, COPY)
-                else:
-                    nc.vector.tensor_copy(target, source)
-            elif step == "tsg":
-                nc.vector.tensor_copy(ts_listed[:], get("Wts")[:].indirect(offsets[:]))
-            elif step[0] == "y":
-                name, j, kind, g = step[:2], int(step[1]), step[2], int(step[3])
-                h, c = divmod(j, 4)
-                if kind == "g":
-                    g1 = span(name, g)
-                    nc.vector.tensor_tensor(
-                        get("dl%d%d" % (j, g))[:],
-                        get("W" + name)[:].indirect(offsets[:, 32 * g : 32 * g1]),
-                        ts_listed[:, 512 * g : 512 * g1],
-                        MULT,
-                    )
-                elif kind == "T":
-                    g0 = g if name in SPLIT else 0
-                    listed = get("dl%d%d" % (j, g0))
-                    banks[step] = turn.tile([P, 4, P], F32, name="turned")
-                    for t in range(4):
-                        first = 512 * (g - g0)
-                        nc.tensor.transpose(banks[step][:, t, :], listed[:, first + t : first + 512 : 4], eye[:])
-                else:
-                    c0 = [z[0] for z in ZGROUPS[h] if z[0] <= c < z[1]][0]
-                    staged = get("zs%d%d%d" % (h, g, c0))
-                    nc.scalar.copy(
-                        staged[:, (c - c0) * P : (c - c0 + 1) * P, :],
-                        banks[name + "T%d" % g][:].rearrange("p t n -> p n t"),
-                    )
-            elif step[:2] == "zq":
-                h, g, c0 = int(step[2]), int(step[3]), int(step[4])
-                c1 = [z[1] for z in ZGROUPS[h] if z[0] == c0][0]
-                cols = slice(c0 * P, c1 * P)
-                nc.vector.quantize_mx(
-                    out=get("zc%d%d" % (h, g))[:, cols].bitcast(E5M2),
-                    scales=z_scales[h][g][:, cols],
-                    in_=get("zs%d%d%d" % (h, g, c0))[:].rearrange("p n t -> p (n t)"),
-                )
-            elif step[0] == "x":
-                name, j, kind, g = step[:2], int(step[1]), step[2], int(step[3])
-                g1 = span(name, g)
-                if kind == "c":
-                    parts = NCAST.get(name, 2)
-                    half = slice(g * T // parts, (g + 1) * T // parts)
-                    if name in CAST_ON_VECTOR:
-                        nc.vector.tensor_copy(get("r%d" % j)[:, half], get("W" + name)[:, half])
-                    else:
-                        nc.scalar.activation(get("r%d" % j)[:, half], get("W" + name)[:, half], COPY)
-                elif kind == "g":
-                    in_list_order = get("xl%d%d" % (j, g))[:].rearrange("p (u s i) -> p s u i", u=2, i=2)
-                    entries = offsets[:, 32 * g : 32 * g1]
-                    if X_GATHER[name][g] == "V":
-                        nc.vector.tensor_copy(in_list_order, get("W" + name)[:].indirect(entries))
-                    else:
-                        nc.scalar.activation(in_list_order, get("r%d" % j)[:].indirect(entries), COPY)
-                elif kind == "T":
-                    words = get("xl%d%d" % (j, g))[:].bitcast(F32).rearrange("p (u g s) -> p u g s", u=2, s=P)
-                    banks[step] = turn.tile([P, 2, 2, P], F32, name="turned")
-                    for q in range(g1 - g):
-                        for u in range(2):
-                            nc.tensor.transpose(banks[step][:, q, u, :], words[:, u, q, :], eye[:])
-                elif kind == "E":
-                    staged = get("xs%d%d" % (j, g))[:].bitcast(F32).rearrange("p (g d u) -> p g d u", d=P, u=2)
-                    nc.scalar.copy(staged, banks[name + "T%d" % g][:, 0 : g1 - g].rearrange("p g u d -> p g d u"))
-                else:
-                    nc.vector.quantize_mx(
-                        out=get("xc%d%d" % (j, g))[:].bitcast(E4M3),
-                        scales=x_scales[j][:, g * P : g1 * P],
-                        in_=get("xs%d%d" % (j, g))[:],
-                    )
-            elif step[:2] == "mm":
-                j, h, g = int(step[2]), int(step[3]), ["a", "b"].index(step[4])
-                if g == 0:
-                    banks[step[2:4]] = sums.tile([P, 512], F32, name="acc")
-                g0 = g if "x%d" % j in SPLIT else 0
-                nc.tensor.matmul_mx(
-                    out=banks[step[2:4]][:],
-                    lhsT=get("xc%d%d" % (j, g0))[:, (g - g0) * P : (g - g0 + 1) * P].bitcast(E4M3),
-                    lhsT_scale=x_scales[j][:, g * P : (g + 1) * P],
-                    rhs=get("zc%d%d" % (h, g))[:].bitcast(E5M2),
-                    rhs_scale=z_scales[h][g][:],
-                    start=(g == 0),
-                    stop=(g == 1),
-                )
-            elif step[:2] == "oe":
-                j, h = int(step[2]), int(step[3])
-                width = 256 if [j, h] in HALVED else 512
-                for c in range(0, 512, width):
-                    if [j, h] in OUT_ON_VECTOR:
-                        nc.vector.tensor_copy(get("o%d%d" % (j, h))[:, c : c + width], banks[step[2:4]][:, c : c + width])
-                    else:
-                        nc.scalar.copy(get("o%d%d" % (j, h))[:, c : c + width], banks[step[2:4]][:, c : c + width])
+        def evacuate(engine, target, source):
+            if engine == "S":
+                nc.scalar.copy(target, source)
             else:
-                j, h = int(step[2]), int(step[3])
-                width = 256 if [j, h] in HALVED else 512
-                for c in range(0, 512, width):
-                    nc.sync.dma_start(
-                        out[0, j * P : (j + 1) * P, h * 512 + c : h * 512 + c + width],
-                        get("o%d%d" % (j, h))[:, c : c + width],
+                nc.vector.tensor_copy(target, source)
+
+        def spread_ts(k, engine):
+            bank = turn.tile([P, 4, P], F32, name="turned")
+            for q in range(4):
+                m = 4 * k + q
+                nc.tensor.transpose(bank[:, q, :], ts_rows[:, m : m + 1].to_broadcast([P, P]), eye[:])
+            target = ts_window[:].rearrange("p (n k q) -> p k n q", k=TS_COLS // 4, q=4)[:, k]
+            if engine == "S":
+                nc.scalar.activation(target, bank[:].rearrange("p q n -> p n q"), COPY)
+            else:
+                nc.vector.tensor_copy(target, bank[:].rearrange("p q n -> p n q"))
+
+        def gather_ts():
+            nc.vector.tensor_copy(ts_listed[:], ts_window[:].indirect(offsets[:]))
+
+        def gather_dy(j, g0, g1, host=None, at=0):
+            held["dy", j, g0] = tile("dy%d%d" % (j, g0), [P, PASS * (g1 - g0)], F32, host, at)
+            nc.vector.tensor_copy(held["dy", j, g0][:], window["y%d" % j][:].indirect(offsets[:, 32 * g0 : 32 * g1]))
+
+        def weigh(j, g0, g1, host=None, at=0):
+            held["dz", j, g0] = tile("dz%d%d" % (j, g0), [P, PASS * (g1 - g0)], BF16, host, at)
+            nc.gpsimd.tensor_tensor(held["dz", j, g0][:], held["dy", j, g0][:], ts_listed[:, PASS * g0 : PASS * g1], MULT)
+
+        def z_staged(j):
+            key = ("zs", j // 4, Z_GROUP[j])
+            if key not in held:
+                width = Z_GROUP[j][1] - Z_GROUP[j][0]
+                held[key] = tile("zs%d_%d" % (j // 4, Z_GROUP[j][0]), [P, 2, width * P, 4], BF16)
+            first = (j % 4 - Z_GROUP[j][0]) * P
+            return held[key][:, :, first : first + P, :]
+
+        def turn_words(key, listed, g0, g1):
+            words = listed[:].bitcast(F32)
+            held[key] = turn.tile([P, 2, 2, P], F32, name="turned")
+            for g in range(g1 - g0):
+                for u in range(2):
+                    nc.tensor.transpose(held[key][:, g, u, :], words[:, 256 * g + u : 256 * (g + 1) : 2], eye[:])
+
+        def turn_dz(j, g0, g1):
+            turn_words(("zb", j, g0), held["dz", j, g0], g0, g1)
+
+        def stage_dz(j, g0, g1, engine="S"):
+            target = z_staged(j)[:, g0:g1].rearrange("p g n t -> p g (n t)").bitcast(F32).rearrange("p g (n u) -> p g n u", u=2)
+            evacuate(engine, target, held["zb", j, g0][:, 0 : g1 - g0].rearrange("p g u n -> p g n u"))
+
+        def gather_dz(j, g0, g1, host=None, at=0):
+            listed = tile("df%d%d" % (j, g0), [P, PASS * (g1 - g0)], F32, host, at)
+            slots = slice(PASS * g0, PASS * g1)
+            for g in range(g0, g1):
+                held["df", j, g] = listed[:, PASS * (g - g0) : PASS * (g - g0 + 1)]
+            nc.vector.tensor_tensor(
+                listed[:], window["y%d" % j][:].indirect(offsets[:, 32 * g0 : 32 * g1]), ts_listed[:, slots], MULT
+            )
+
+        def turn_dz32(j, g):
+            held["zb", j, g] = turn.tile([P, 4, P], F32, name="turned")
+            for t in range(4):
+                nc.tensor.transpose(held["zb", j, g][:, t, :], held["df", j, g][:, t:PASS:4], eye[:])
+
+        def stage_dz32(j, g, engine="S"):
+            evacuate(engine, z_staged(j)[:, g], held["zb", j, g][:].rearrange("p t n -> p n t"))
+
+        def quantize_dz(h, c0, c1, host=None, at=0):
+            if ("zc", h) not in held:
+                held["zc", h] = tile("zc%d" % h, [P, 2 * PASS], U32, host, at)
+            staged = held["zs", h, (c0, c1)]
+            if c1 - c0 == 4:
+                nc.vector.quantize_mx(
+                    out=held["zc", h][:].bitcast(E5M2), scales=z_scales[h][:], in_=staged[:].rearrange("p g n t -> p (g n t)")
+                )
+            else:
+                for g in range(2):
+                    cols = slice(PASS * g + c0 * P, PASS * g + c1 * P)
+                    nc.vector.quantize_mx(
+                        out=held["zc", h][:, cols].bitcast(E5M2),
+                        scales=z_scales[h][:, cols],
+                        in_=staged[:, g].rearrange("p n t -> p (n t)"),
                     )
+
+        def round_x(j, k, parts, host=None, at=0):
+            if ("xr", j) not in held:
+                held["xr", j] = tile("xr%d" % j, [P, T], BF16, host, at)
+            cols = slice(k * T // parts, (k + 1) * T // parts)
+            nc.scalar.activation(held["xr", j][:, cols], window["x%d" % j][:, cols], COPY)
+
+        def gather_x(j, g0, g1, engine, host=None, at=0):
+            held["xl", j, g0] = tile("xl%d%d" % (j, g0), [P, PASS * (g1 - g0)], BF16, host, at)
+            entries = offsets[:, 32 * g0 : 32 * g1]
+            if engine == "S":
+                nc.scalar.activation(held["xl", j, g0][:], held["xr", j][:].indirect(entries), COPY)
+            else:
+                nc.vector.tensor_copy(held["xl", j, g0][:], window["x%d" % j][:].indirect(entries))
+
+        def turn_x(j, g0, g1):
+            turn_words(("xb", j, g0), held["xl", j, g0], g0, g1)
+
+        def stage_x(j, g0, g1, engine="S", host=None, at=0):
+            held["xs", j, g0] = tile("xs%d%d" % (j, g0), [P, PASS * (g1 - g0)], BF16, host, at)
+            target = held["xs", j, g0][:].bitcast(F32).rearrange("p (g d u) -> p g d u", d=P, u=2)
+            evacuate(engine, target, held["xb", j, g0][:, 0 : g1 - g0].rearrange("p g u d -> p g d u"))
+
+        def quantize_x(j, g0, g1, host=None, at=0):
+            codes = tile("xc%d%d" % (j, g0), [P, P * (g1 - g0)], U32, host, at)
+            for g in range(g0, g1):
+                held["xc", j, g] = codes[:, (g - g0) * P : (g - g0 + 1) * P]
+            nc.vector.quantize_mx(out=codes[:].bitcast(E4M3), scales=x_scales[j][:, g0 * P : g1 * P], in_=held["xs", j, g0][:])
+
+        def multiply(j, h, g):
+            if g == 0:
+                held["acc", j, h] = sums.tile([P, PASS], F32, name="acc")
+            nc.tensor.matmul_mx(
+                out=held["acc", j, h][:],
+                lhsT=held["xc", j, g].bitcast(E4M3),
+                lhsT_scale=x_scales[j][:, g * P : (g + 1) * P],
+                rhs=held["zc", h][:, PASS * g : PASS * (g + 1)].bitcast(E5M2),
+                rhs_scale=z_scales[h][:, PASS * g : PASS * (g + 1)],
+                start=(g == 0),
+                stop=(g == 1),
+            )
+
+        def put_out(j, h, engine, parts=1, host=None, at=0):
+            result = tile("out%d%d" % (j, h), [P, PASS], F32, host, at)
+            for k in range(parts):
+                cols = slice(k * PASS // parts, (k + 1) * PASS // parts)
+                evacuate(engine, result[:, cols], held["acc", j, h][:, cols])
+                nc.sync.dma_start(out[0, j * P : (j + 1) * P, h * PASS + cols.start : h * PASS + cols.stop], result[:, cols])
+
+        for k in range(4):
+            spread_ts(k, "S")
+        gather_dy(0, 0, 2)
+        gather_ts()
+        round_x(0, 0, 1, "rows")
+        gather_x(0, 0, 2, "S")
+        weigh(0, 0, 2)
+        gather_dy(1, 0, 2, "ts")
+        turn_x(0, 0, 2)
+        stage_x(0, 0, 2)
+        turn_dz(0, 0, 2)
+        stage_dz(0, 0, 2)
+        for j in (1, 2, 3):
+            weigh(j, 0, 2)
+            gather_dy(j + 1, 0, 2, "y%d" % j)
+            turn_dz(j, 0, 2)
+            stage_dz(j, 0, 2)
+        weigh(4, 0, 2)
+        quantize_x(0, 0, 2, "y4")
+        round_x(1, 0, 1)
+        quantize_dz(0, 0, 4, "y4", 4096)
+        turn_dz(4, 0, 2)
+        stage_dz(4, 0, 2)
+        gather_x(1, 0, 2, "S")
+        multiply(0, 0, 0)
+        multiply(0, 0, 1)
+        for j in (5, 6, 7):
+            for g in range(2):
+                gather_dy(j, g, g + 1, None if j == 5 else "y%d" % (j - 1), 2048 * g)
+                weigh(j, g, g + 1)
+                if j == 5 and g == 1:
+                    turn_x(1, 0, 2)
+                    stage_x(1, 0, 2)
+                    put_out(0, 0, "S")
+                if j == 7:
+                    round_x(2, g, 2)
+                turn_dz(j, g, g + 1)
+                stage_dz(j, g, g + 1)
+        quantize_x(1, 0, 2, "y7")
+        gather_x(2, 0, 2, "S")
+        quantize_dz(1, 0, 2, "y7", 4096)
+        multiply(1, 0, 0)
+        multiply(1, 0, 1)
+        gather_x(3, 0, 1, "V")
+        quantize_dz(1, 2, 4)
+        gather_x(3, 1, 2, "V")
+        for j in range(2):
+            multiply(j, 1, 0)
+            multiply(j, 1, 1)
+        turn_x(3, 0, 1)
+        turn_x(2, 0, 2)
+        turn_x(3, 1, 2)
+        stage_x(3, 0, 1)
+        stage_x(2, 0, 2)
+        put_out(1, 0, "S")
+        stage_x(3, 1, 2)
+        quantize_x(2, 0, 2, "x3", 4096)
+        quantize_x(3, 0, 1)
+        put_out(0, 1, "V", 1, "x3", 0)
+        quantize_x(3, 1, 2)
+        put_out(1, 1, "V", 1, "x3", 2048)
+        multiply(2, 0, 0)
+        multiply(2, 0, 1)
+        multiply(2, 1, 0)
+        multiply(2, 1, 1)
+        multiply(3, 0, 0)
+        multiply(3, 1, 0)
+        multiply(3, 0, 1)
+        multiply(3, 1, 1)
+        put_out(2, 0, "S")
+        put_out(2, 1, "V")
+        put_out(3, 0, "S", 2)
+        put_out(3, 1, "V", 2)

@@ -18,12 +18,12 @@ MULT = mybir.AluOpType.mult
 
 P = 128
 PASS = 512
-TS_COLS = T // P
 WINDOW_BYTES = 4 * T
-ARRIVAL = ["y0","x0","y1","y2","y3","y4","x1","y5","y6","y7","x2","x3"]
-Z_GROUP = [(0, 4)] * 4 + [(0, 2)] * 2 + [(2, 4)] * 2
+ARRIVAL = ["x0","y0","x1","y1","y2","y3","y4","x2","y5","y6","y7","x3"]
 HOSTS = ARRIVAL + ["ts", "rows"]
-HALVED_LOADS = ["x2"]
+PLACE = {name: k * WINDOW_BYTES for k, name in enumerate(HOSTS)} | {"a%d" % j: len(HOSTS) * WINDOW_BYTES + 4096 * j for j in range(8)}
+TURNING_BANKS = 4
+HALVED_LOADS = []
 
 
 def tile_attend_gex_w_kernel(tc, xT, dyT, ts, offs, out):
@@ -31,17 +31,17 @@ def tile_attend_gex_w_kernel(tc, xT, dyT, ts, offs, out):
     with ExitStack() as ctx:
         keep = ctx.enter_context(tc.tile_pool(name="keep", bufs=1))
         arena = ctx.enter_context(tc.tile_pool(name="arena", bufs=1))
-        turn = ctx.enter_context(tc.psum_pool(name="turn", bufs=4))
-        sums = ctx.enter_context(tc.psum_pool(name="sums", bufs=4))
+        psum = ctx.enter_context(tc.psum_pool(name="psum", bufs=1))
 
         def tile(name, shape, dtype, host=None, at=0):
             if host is None:
                 return keep.tile(shape, dtype, name=name, align_bytes=64)
-            return arena.tile(shape, dtype, name=name, align_bytes=64, offset=HOSTS.index(host) * WINDOW_BYTES + at)
+            return arena.tile(shape, dtype, name=name, align_bytes=64, offset=PLACE[host] + at)
 
         offsets = keep.tile([P, N // 16], U16, name="offsets")
         eye = tile("eye", [P, P], F32)
-        ts_rows = tile("ts_rows", [P, TS_COLS], F32, "rows")
+        ts_row = tile("ts_row", [P, N], F32, "rows")
+        ts_cols = [tile("ts_cols%d" % g, [P, 4], F32, "a%d" % (6 + g)) for g in range(2)]
         ts_window = tile("ts_window", [P, T], F32, "ts")
         ts_listed = tile("ts_listed", [P, N], F32)
         window = {name: tile("window_" + name, [P, T], F32, host=name) for name in ARRIVAL}
@@ -49,8 +49,10 @@ def tile_attend_gex_w_kernel(tc, xT, dyT, ts, offs, out):
         x_scales = [tile("x_scales%d" % j, [P, 2 * P], U8) for j in range(4)]
         held = {}
 
-        nc.sync.dma_start(ts_rows[:], ts[0:1, :].rearrange("o (n m) -> (o n) m", m=TS_COLS))
+        nc.vector.memset(ts_window[0 : P - 1, 0 : T // 2], 0.0)
+        nc.gpsimd.memset(ts_window[0 : P - 1, T // 2 : T], 0.0)
         nc.sync.dma_start(offsets[:], offs)
+        nc.sync.dma_start(ts_window[P - 1 : P, :], ts[0:1, :])
         for name in ARRIVAL:
             j = int(name[1])
             source = xT if name[0] == "x" else dyT
@@ -60,25 +62,34 @@ def tile_attend_gex_w_kernel(tc, xT, dyT, ts, offs, out):
                 nc.sync.dma_start(window[name][:, cols], source[j * P : (j + 1) * P, cols])
         make_identity(nc, eye[:])
 
+        def bank_tile(shape, bank):
+            held["banks"] = held.get("banks", 0) + 1
+            return psum.tile(shape, F32, name="bank_use%d" % held["banks"], offset=2048 * bank)
+
+        def next_turning_bank(shape, bank=None):
+            if bank is None:
+                held["turns"] = held.get("turns", -1) + 1
+                bank = held["turns"] % TURNING_BANKS
+            return bank_tile(shape, bank)
+
         def evacuate(engine, target, source):
             if engine == "S":
                 nc.scalar.copy(target, source)
             else:
                 nc.vector.tensor_copy(target, source)
 
-        def spread_ts(k, engine):
-            bank = turn.tile([P, 4, P], F32, name="turned")
-            for q in range(4):
-                m = 4 * k + q
-                nc.tensor.transpose(bank[:, q, :], ts_rows[:, m : m + 1].to_broadcast([P, P]), eye[:])
-            target = ts_window[:].rearrange("p (n k q) -> p k n q", k=TS_COLS // 4, q=4)[:, k]
-            if engine == "S":
-                nc.scalar.activation(target, bank[:].rearrange("p q n -> p n q"), COPY)
-            else:
-                nc.vector.tensor_copy(target, bank[:].rearrange("p q n -> p n q"))
+        def gather_ts(g):
+            nc.vector.tensor_copy(ts_row[:, PASS * g : PASS * (g + 1)], ts_window[:].indirect(offsets[:, 32 * g : 32 * (g + 1)]))
 
-        def gather_ts():
-            nc.vector.tensor_copy(ts_listed[:], ts_window[:].indirect(offsets[:]))
+        def spread_ts(g):
+            bank = next_turning_bank([P, 4, P])
+            for c in range(4):
+                nc.tensor.transpose(bank[:, c, :], ts_row[:, PASS * g + P * c : PASS * g + P * (c + 1)], eye[:])
+            nc.vector.tensor_copy(ts_cols[g][:], bank[:, :, P - 1])
+            bank = next_turning_bank([P, 4, P])
+            for c in range(4):
+                nc.tensor.transpose(bank[:, c, :], ts_cols[g][:, c : c + 1].to_broadcast([P, P]), eye[:])
+            nc.vector.tensor_copy(ts_listed[:, PASS * g : PASS * (g + 1)], bank[:].rearrange("p c n -> p (c n)"))
 
         def gather_dy(j, g0, g1, host=None, at=0):
             held["dy", j, g0] = tile("dy%d%d" % (j, g0), [P, PASS * (g1 - g0)], F32, host, at)
@@ -88,61 +99,54 @@ def tile_attend_gex_w_kernel(tc, xT, dyT, ts, offs, out):
             held["dz", j, g0] = tile("dz%d%d" % (j, g0), [P, PASS * (g1 - g0)], BF16, host, at)
             nc.gpsimd.tensor_tensor(held["dz", j, g0][:], held["dy", j, g0][:], ts_listed[:, PASS * g0 : PASS * g1], MULT)
 
-        def z_staged(j):
-            key = ("zs", j // 4, Z_GROUP[j])
-            if key not in held:
-                width = Z_GROUP[j][1] - Z_GROUP[j][0]
-                held[key] = tile("zs%d_%d" % (j // 4, Z_GROUP[j][0]), [P, 2, width * P, 4], BF16)
-            first = (j % 4 - Z_GROUP[j][0]) * P
-            return held[key][:, :, first : first + P, :]
-
-        def turn_words(key, listed, g0, g1):
+        def turn_words(key, listed, g0, g1, bank):
             words = listed[:].bitcast(F32)
-            held[key] = turn.tile([P, 2, 2, P], F32, name="turned")
+            held[key] = next_turning_bank([P, 2, 2, P], bank)
             for g in range(g1 - g0):
                 for u in range(2):
                     nc.tensor.transpose(held[key][:, g, u, :], words[:, 256 * g + u : 256 * (g + 1) : 2], eye[:])
 
-        def turn_dz(j, g0, g1):
-            turn_words(("zb", j, g0), held["dz", j, g0], g0, g1)
+        def turn_dz(j, g, fresh, bank=None):
+            if fresh:
+                held["zb", j] = next_turning_bank([P, 2, 2, P], bank)
+            words = held["dz", j, g][:].bitcast(F32)
+            for u in range(2):
+                nc.tensor.transpose(held["zb", j][:, g, u, :], words[:, u:256:2], eye[:])
+
+        def z_staged(j):
+            h, c = divmod(j, 4)
+            if ("zs", h) not in held:
+                held["zs", h] = tile("zs%d" % h, [P, 2, PASS, 4], BF16, "ts" if h == 0 else None)
+            return held["zs", h][:, :, c * P : (c + 1) * P, :]
 
         def stage_dz(j, g0, g1, engine="S"):
             target = z_staged(j)[:, g0:g1].rearrange("p g n t -> p g (n t)").bitcast(F32).rearrange("p g (n u) -> p g n u", u=2)
-            evacuate(engine, target, held["zb", j, g0][:, 0 : g1 - g0].rearrange("p g u n -> p g n u"))
+            evacuate(engine, target, held["zb", j][:, g0:g1].rearrange("p g u n -> p g n u"))
 
         def gather_dz(j, g0, g1, host=None, at=0):
             listed = tile("df%d%d" % (j, g0), [P, PASS * (g1 - g0)], F32, host, at)
-            slots = slice(PASS * g0, PASS * g1)
             for g in range(g0, g1):
                 held["df", j, g] = listed[:, PASS * (g - g0) : PASS * (g - g0 + 1)]
             nc.vector.tensor_tensor(
-                listed[:], window["y%d" % j][:].indirect(offsets[:, 32 * g0 : 32 * g1]), ts_listed[:, slots], MULT
+                listed[:], window["y%d" % j][:].indirect(offsets[:, 32 * g0 : 32 * g1]), ts_listed[:, PASS * g0 : PASS * g1], MULT
             )
 
-        def turn_dz32(j, g):
-            held["zb", j, g] = turn.tile([P, 4, P], F32, name="turned")
+        def turn_dz32(j, g, bank=None):
+            held["zb", j, g] = next_turning_bank([P, 4, P], bank)
             for t in range(4):
                 nc.tensor.transpose(held["zb", j, g][:, t, :], held["df", j, g][:, t:PASS:4], eye[:])
 
         def stage_dz32(j, g, engine="S"):
             evacuate(engine, z_staged(j)[:, g], held["zb", j, g][:].rearrange("p t n -> p n t"))
 
-        def quantize_dz(h, c0, c1, host=None, at=0):
-            if ("zc", h) not in held:
-                held["zc", h] = tile("zc%d" % h, [P, 2 * PASS], U32, host, at)
-            staged = held["zs", h, (c0, c1)]
-            if c1 - c0 == 4:
-                nc.vector.quantize_mx(
-                    out=held["zc", h][:].bitcast(E5M2), scales=z_scales[h][:], in_=staged[:].rearrange("p g n t -> p (g n t)")
-                )
-            else:
-                for g in range(2):
-                    cols = slice(PASS * g + c0 * P, PASS * g + c1 * P)
-                    nc.vector.quantize_mx(
-                        out=held["zc", h][:, cols].bitcast(E5M2),
-                        scales=z_scales[h][:, cols],
-                        in_=staged[:, g].rearrange("p n t -> p (n t)"),
-                    )
+        def quantize_dz(h, g, c0, c1, host=None, at=0):
+            if ("zc", h, g) not in held:
+                held["zc", h, g] = tile("zc%d%d" % (h, g), [P, PASS], U32, host, at)
+            nc.vector.quantize_mx(
+                out=held["zc", h, g][:, c0 * P : c1 * P].bitcast(E5M2),
+                scales=z_scales[h][:, PASS * g + c0 * P : PASS * g + c1 * P],
+                in_=held["zs", h][:, g, c0 * P : c1 * P, :].rearrange("p n t -> p (n t)"),
+            )
 
         def round_x(j, k, parts, host=None, at=0):
             if ("xr", j) not in held:
@@ -158,28 +162,31 @@ def tile_attend_gex_w_kernel(tc, xT, dyT, ts, offs, out):
             else:
                 nc.vector.tensor_copy(held["xl", j, g0][:], window["x%d" % j][:].indirect(entries))
 
-        def turn_x(j, g0, g1):
-            turn_words(("xb", j, g0), held["xl", j, g0], g0, g1)
+        def turn_x(j, g0, g1, bank=None):
+            turn_words(("xb", j, g0), held["xl", j, g0], g0, g1, bank)
 
-        def stage_x(j, g0, g1, engine="S", host=None, at=0):
-            held["xs", j, g0] = tile("xs%d%d" % (j, g0), [P, PASS * (g1 - g0)], BF16, host, at)
-            target = held["xs", j, g0][:].bitcast(F32).rearrange("p (g d u) -> p g d u", d=P, u=2)
-            evacuate(engine, target, held["xb", j, g0][:, 0 : g1 - g0].rearrange("p g u d -> p g d u"))
+        def stage_x(j, g, engine="S"):
+            if ("xs", j) not in held:
+                held["xs", j] = tile("xs%d" % j, [P, N], BF16, "a%d" % j)
+            target = held["xs", j][:, PASS * g : PASS * (g + 1)].bitcast(F32).rearrange("p (d u) -> p d u", u=2)
+            evacuate(engine, target, held["xb", j, g][:, 0].rearrange("p u d -> p d u"))
 
         def quantize_x(j, g0, g1, host=None, at=0):
             codes = tile("xc%d%d" % (j, g0), [P, P * (g1 - g0)], U32, host, at)
             for g in range(g0, g1):
                 held["xc", j, g] = codes[:, (g - g0) * P : (g - g0 + 1) * P]
-            nc.vector.quantize_mx(out=codes[:].bitcast(E4M3), scales=x_scales[j][:, g0 * P : g1 * P], in_=held["xs", j, g0][:])
+            nc.vector.quantize_mx(
+                out=codes[:].bitcast(E4M3), scales=x_scales[j][:, g0 * P : g1 * P], in_=held["xs", j][:, PASS * g0 : PASS * g1]
+            )
 
-        def multiply(j, h, g):
+        def multiply(j, h, g, bank=None):
             if g == 0:
-                held["acc", j, h] = sums.tile([P, PASS], F32, name="acc")
+                held["acc", j, h] = bank_tile([P, PASS], bank)
             nc.tensor.matmul_mx(
                 out=held["acc", j, h][:],
                 lhsT=held["xc", j, g].bitcast(E4M3),
                 lhsT_scale=x_scales[j][:, g * P : (g + 1) * P],
-                rhs=held["zc", h][:, PASS * g : PASS * (g + 1)].bitcast(E5M2),
+                rhs=held["zc", h, g][:].bitcast(E5M2),
                 rhs_scale=z_scales[h][:, PASS * g : PASS * (g + 1)],
                 start=(g == 0),
                 stop=(g == 1),
@@ -192,76 +199,69 @@ def tile_attend_gex_w_kernel(tc, xT, dyT, ts, offs, out):
                 evacuate(engine, result[:, cols], held["acc", j, h][:, cols])
                 nc.sync.dma_start(out[0, j * P : (j + 1) * P, h * PASS + cols.start : h * PASS + cols.stop], result[:, cols])
 
-        for k in range(4):
-            spread_ts(k, "S")
-        gather_dy(0, 0, 2)
-        gather_ts()
-        round_x(0, 0, 1, "rows")
-        gather_x(0, 0, 2, "S")
-        weigh(0, 0, 2)
-        gather_dy(1, 0, 2, "ts")
-        turn_x(0, 0, 2)
-        stage_x(0, 0, 2)
-        turn_dz(0, 0, 2)
-        stage_dz(0, 0, 2)
-        for j in (1, 2, 3):
-            weigh(j, 0, 2)
-            gather_dy(j + 1, 0, 2, "y%d" % j)
-            turn_dz(j, 0, 2)
-            stage_dz(j, 0, 2)
-        weigh(4, 0, 2)
-        quantize_x(0, 0, 2, "y4")
-        round_x(1, 0, 1)
-        quantize_dz(0, 0, 4, "y4", 4096)
-        turn_dz(4, 0, 2)
-        stage_dz(4, 0, 2)
-        gather_x(1, 0, 2, "S")
-        multiply(0, 0, 0)
-        multiply(0, 0, 1)
-        for j in (5, 6, 7):
+        def dy_back(j, banks):
             for g in range(2):
-                gather_dy(j, g, g + 1, None if j == 5 else "y%d" % (j - 1), 2048 * g)
-                weigh(j, g, g + 1)
-                if j == 5 and g == 1:
-                    turn_x(1, 0, 2)
-                    stage_x(1, 0, 2)
-                    put_out(0, 0, "S")
-                if j == 7:
-                    round_x(2, g, 2)
-                turn_dz(j, g, g + 1)
-                stage_dz(j, g, g + 1)
-        quantize_x(1, 0, 2, "y7")
-        gather_x(2, 0, 2, "S")
-        quantize_dz(1, 0, 2, "y7", 4096)
-        multiply(1, 0, 0)
-        multiply(1, 0, 1)
-        gather_x(3, 0, 1, "V")
-        quantize_dz(1, 2, 4)
-        gather_x(3, 1, 2, "V")
+                turn_dz32(j, g, banks[g])
+                stage_dz32(j, g)
+
+        def x_on_scalar(j):
+            round_x(j, 0, 1)
+            for g in range(2):
+                gather_x(j, g, g + 1, "V" if (j, g) == (0, 0) else "S")
+            for g in range(2):
+                turn_x(j, g, g + 1, 6 + g)
+                stage_x(j, g)
+
+        for g in range(2):
+            gather_ts(g)
+        for g in range(2):
+            spread_ts(g)
+        x_on_scalar(0)
+        for g in range(2):
+            gather_dz(0, g, g + 1)
+        quantize_x(0, 0, 2, "y0")
+        x_on_scalar(1)
+        dy_back(0, (6, 7))
+        for j in range(1, 4):
+            gather_dz(j, 0, 2)
+            dy_back(j, (0, 1) if j % 2 else (2, 3))
+        gather_dz(4, 0, 2)
+        quantize_x(1, 0, 2, "y4", 4096)
+        for g in range(2):
+            quantize_dz(0, g, 0, 4, "y4", 2048 * g)
         for j in range(2):
-            multiply(j, 1, 0)
-            multiply(j, 1, 1)
-        turn_x(3, 0, 1)
-        turn_x(2, 0, 2)
-        turn_x(3, 1, 2)
-        stage_x(3, 0, 1)
-        stage_x(2, 0, 2)
-        put_out(1, 0, "S")
-        stage_x(3, 1, 2)
-        quantize_x(2, 0, 2, "x3", 4096)
-        quantize_x(3, 0, 1)
-        put_out(0, 1, "V", 1, "x3", 0)
-        quantize_x(3, 1, 2)
-        put_out(1, 1, "V", 1, "x3", 2048)
-        multiply(2, 0, 0)
-        multiply(2, 0, 1)
-        multiply(2, 1, 0)
-        multiply(2, 1, 1)
-        multiply(3, 0, 0)
-        multiply(3, 1, 0)
-        multiply(3, 0, 1)
-        multiply(3, 1, 1)
+            for g in range(2):
+                multiply(j, 0, g, 4 + j)
+        x_on_scalar(2)
+        dy_back(4, (6, 7))
+        for j in range(5, 7):
+            gather_dz(j, 0, 2)
+            dy_back(j, (0, 1) if j % 2 else (2, 3))
+        gather_dz(7, 0, 1)
+        gather_dz(7, 1, 2, "a5")
+        dy_back(7, (0, 1))
+        quantize_x(2, 0, 2, "y7")
+        for g in range(2):
+            quantize_dz(1, g, 0, 4, "y7", 2048 + 2048 * g)
+        for g in range(2):
+            multiply(2, 0, g, 2)
+        for g in range(2):
+            for j in range(3):
+                multiply(j, 1, g, (3, 0, 6)[j])
+        put_out(0, 0, "S", 1, "a5")
+        put_out(1, 0, "S", 1, "y7", 6144)
         put_out(2, 0, "S")
-        put_out(2, 1, "V")
-        put_out(3, 0, "S", 2)
-        put_out(3, 1, "V", 2)
+        for g in range(2):
+            gather_x(3, g, g + 1, "V")
+            turn_x(3, g, g + 1, (1, 7)[g])
+            stage_x(3, g)
+        quantize_x(3, 0, 1, "x3")
+        put_out(0, 1, "S")
+        put_out(1, 1, "V", 1, "x3", 2048)
+        put_out(2, 1, "V", 1, "x3", 4096)
+        quantize_x(3, 1, 2)
+        for g in range(2):
+            for h in range(2):
+                multiply(3, h, g, 4 + h)
+        put_out(3, 0, "V", 2)
+        put_out(3, 1, "S", 2)

@@ -18,12 +18,7 @@ MULT = mybir.AluOpType.mult
 
 P = 128
 PASS = 512
-WINDOW_BYTES = 4 * T
-ARRIVAL = ["x0","y0","x1","y1","y2","y3","y4","x2","y5","y6","y7","x3"]
-HOSTS = ARRIVAL + ["ts", "rows"]
-PLACE = {name: k * WINDOW_BYTES for k, name in enumerate(HOSTS)} | {"a%d" % j: len(HOSTS) * WINDOW_BYTES + 4096 * j for j in range(8)}
-TURNING_BANKS = 4
-HALVED_LOADS = []
+ARRIVAL = ["x0", "y0", "y1", "x1", "y2", "y3", "y4", "y5", "y6", "y7", "x2", "x3"]
 
 
 def tile_attend_gex_w_kernel(tc, xT, dyT, ts, offs, out):
@@ -32,236 +27,222 @@ def tile_attend_gex_w_kernel(tc, xT, dyT, ts, offs, out):
         keep = ctx.enter_context(tc.tile_pool(name="keep", bufs=1))
         arena = ctx.enter_context(tc.tile_pool(name="arena", bufs=1))
         psum = ctx.enter_context(tc.psum_pool(name="psum", bufs=1))
-
-        def tile(name, shape, dtype, host=None, at=0):
-            if host is None:
-                return keep.tile(shape, dtype, name=name, align_bytes=64)
-            return arena.tile(shape, dtype, name=name, align_bytes=64, offset=PLACE[host] + at)
-
-        offsets = keep.tile([P, N // 16], U16, name="offsets")
-        eye = tile("eye", [P, P], F32)
-        ts_row = tile("ts_row", [P, N], F32, "rows")
-        ts_cols = [tile("ts_cols%d" % g, [P, 4], F32, "a%d" % (6 + g)) for g in range(2)]
-        ts_window = tile("ts_window", [P, T], F32, "ts")
-        ts_listed = tile("ts_listed", [P, N], F32)
-        window = {name: tile("window_" + name, [P, T], F32, host=name) for name in ARRIVAL}
-        z_scales = [tile("z_scales%d" % h, [P, 2 * PASS], U8) for h in range(2)]
-        x_scales = [tile("x_scales%d" % j, [P, 2 * P], U8) for j in range(4)]
+        place = {"end": 0}
         held = {}
 
-        nc.vector.memset(ts_window[0 : P - 1, 0 : T // 2], 0.0)
-        nc.gpsimd.memset(ts_window[0 : P - 1, T // 2 : T], 0.0)
+        def tile(name, columns, dtype, nbytes, host=None, at=0):
+            if host is None:
+                place[name] = place["end"]
+                place["end"] = place["end"] + nbytes
+            else:
+                place[name] = place[host] + at
+            held[name] = arena.tile([P, columns], dtype, name=name, align_bytes=64, offset=place[name])
+            return held[name]
+
+        def bank_tile(name, bank):
+            held[name] = psum.tile([P, PASS], F32, name=name, offset=2048 * bank)
+            return held[name]
+
+        offsets = keep.tile([P, N // 16], U16, name="offsets")
+        eye = tile("eye", P, F32, 4 * P)
+        ts_window = tile("ts_window", T, F32, 4 * T)
+        ts_cols = tile("ts_cols", 8, F32, 64)
+        z_codes = [tile("z_codes%d" % g, DV, U32, 4 * DV) for g in range(2)]
+        z_scales = [tile("z_scales%d" % g, DV, U8, DV) for g in range(2)]
+        x_scales = [tile("x_scales%d" % j, 2 * P, U8, 2 * P) for j in range(4)]
+
+        nc.vector.memset(ts_window[0 : P - 1, :], 0.0)
         nc.sync.dma_start(offsets[:], offs)
-        nc.sync.dma_start(ts_window[P - 1 : P, :], ts[0:1, :])
+        nc.scalar.dma_start(ts_window[P - 1 : P, :], ts[0:1, :])
         for name in ARRIVAL:
             j = int(name[1])
             source = xT if name[0] == "x" else dyT
-            parts = 2 if name in HALVED_LOADS else 1
-            for k in range(parts):
-                cols = slice(k * T // parts, (k + 1) * T // parts)
-                nc.sync.dma_start(window[name][:, cols], source[j * P : (j + 1) * P, cols])
+            nc.sync.dma_start(tile(name, T, F32, 4 * T)[:], source[j * P : (j + 1) * P, :])
         make_identity(nc, eye[:])
 
-        def bank_tile(shape, bank):
-            held["banks"] = held.get("banks", 0) + 1
-            return psum.tile(shape, F32, name="bank_use%d" % held["banks"], offset=2048 * bank)
+        def entries(s0, s1):
+            return offsets[:, s0 // 16 : s1 // 16]
 
-        def next_turning_bank(shape, bank=None):
-            if bank is None:
-                held["turns"] = held.get("turns", -1) + 1
-                bank = held["turns"] % TURNING_BANKS
-            return bank_tile(shape, bank)
-
-        def evacuate(engine, target, source):
+        def copy(engine, target, source):
             if engine == "S":
                 nc.scalar.copy(target, source)
             else:
                 nc.vector.tensor_copy(target, source)
 
-        def gather_ts(g):
-            nc.vector.tensor_copy(ts_row[:, PASS * g : PASS * (g + 1)], ts_window[:].indirect(offsets[:, 32 * g : 32 * (g + 1)]))
-
-        def spread_ts(g):
-            bank = next_turning_bank([P, 4, P])
-            for c in range(4):
-                nc.tensor.transpose(bank[:, c, :], ts_row[:, PASS * g + P * c : PASS * g + P * (c + 1)], eye[:])
-            nc.vector.tensor_copy(ts_cols[g][:], bank[:, :, P - 1])
-            bank = next_turning_bank([P, 4, P])
-            for c in range(4):
-                nc.tensor.transpose(bank[:, c, :], ts_cols[g][:, c : c + 1].to_broadcast([P, P]), eye[:])
-            nc.vector.tensor_copy(ts_listed[:, PASS * g : PASS * (g + 1)], bank[:].rearrange("p c n -> p (c n)"))
-
-        def gather_dy(j, g0, g1, host=None, at=0):
-            held["dy", j, g0] = tile("dy%d%d" % (j, g0), [P, PASS * (g1 - g0)], F32, host, at)
-            nc.vector.tensor_copy(held["dy", j, g0][:], window["y%d" % j][:].indirect(offsets[:, 32 * g0 : 32 * g1]))
-
-        def weigh(j, g0, g1, host=None, at=0):
-            held["dz", j, g0] = tile("dz%d%d" % (j, g0), [P, PASS * (g1 - g0)], BF16, host, at)
-            nc.gpsimd.tensor_tensor(held["dz", j, g0][:], held["dy", j, g0][:], ts_listed[:, PASS * g0 : PASS * g1], MULT)
-
-        def turn_words(key, listed, g0, g1, bank):
-            words = listed[:].bitcast(F32)
-            held[key] = next_turning_bank([P, 2, 2, P], bank)
-            for g in range(g1 - g0):
-                for u in range(2):
-                    nc.tensor.transpose(held[key][:, g, u, :], words[:, 256 * g + u : 256 * (g + 1) : 2], eye[:])
-
-        def turn_dz(j, g, fresh, bank=None):
-            if fresh:
-                held["zb", j] = next_turning_bank([P, 2, 2, P], bank)
-            words = held["dz", j, g][:].bitcast(F32)
-            for u in range(2):
-                nc.tensor.transpose(held["zb", j][:, g, u, :], words[:, u:256:2], eye[:])
-
-        def z_staged(j):
-            h, c = divmod(j, 4)
-            if ("zs", h) not in held:
-                held["zs", h] = tile("zs%d" % h, [P, 2, PASS, 4], BF16, "ts" if h == 0 else None)
-            return held["zs", h][:, :, c * P : (c + 1) * P, :]
-
-        def stage_dz(j, g0, g1, engine="S"):
-            target = z_staged(j)[:, g0:g1].rearrange("p g n t -> p g (n t)").bitcast(F32).rearrange("p g (n u) -> p g n u", u=2)
-            evacuate(engine, target, held["zb", j][:, g0:g1].rearrange("p g u n -> p g n u"))
-
-        def gather_dz(j, g0, g1, host=None, at=0):
-            listed = tile("df%d%d" % (j, g0), [P, PASS * (g1 - g0)], F32, host, at)
-            for g in range(g0, g1):
-                held["df", j, g] = listed[:, PASS * (g - g0) : PASS * (g - g0 + 1)]
-            nc.vector.tensor_tensor(
-                listed[:], window["y%d" % j][:].indirect(offsets[:, 32 * g0 : 32 * g1]), ts_listed[:, PASS * g0 : PASS * g1], MULT
-            )
-
-        def turn_dz32(j, g, bank=None):
-            held["zb", j, g] = next_turning_bank([P, 4, P], bank)
-            for t in range(4):
-                nc.tensor.transpose(held["zb", j, g][:, t, :], held["df", j, g][:, t:PASS:4], eye[:])
-
-        def stage_dz32(j, g, engine="S"):
-            evacuate(engine, z_staged(j)[:, g], held["zb", j, g][:].rearrange("p t n -> p n t"))
-
-        def quantize_dz(h, g, c0, c1, host=None, at=0):
-            if ("zc", h, g) not in held:
-                held["zc", h, g] = tile("zc%d%d" % (h, g), [P, PASS], U32, host, at)
-            nc.vector.quantize_mx(
-                out=held["zc", h, g][:, c0 * P : c1 * P].bitcast(E5M2),
-                scales=z_scales[h][:, PASS * g + c0 * P : PASS * g + c1 * P],
-                in_=held["zs", h][:, g, c0 * P : c1 * P, :].rearrange("p n t -> p (n t)"),
-            )
-
-        def round_x(j, k, parts, host=None, at=0):
-            if ("xr", j) not in held:
-                held["xr", j] = tile("xr%d" % j, [P, T], BF16, host, at)
-            cols = slice(k * T // parts, (k + 1) * T // parts)
-            nc.scalar.activation(held["xr", j][:, cols], window["x%d" % j][:, cols], COPY)
-
-        def gather_x(j, g0, g1, engine, host=None, at=0):
-            held["xl", j, g0] = tile("xl%d%d" % (j, g0), [P, PASS * (g1 - g0)], BF16, host, at)
-            entries = offsets[:, 32 * g0 : 32 * g1]
+        def gather_f32(window, g, engine, host=None, at=0):
+            name = "%s_listed%d" % (window, g)
+            listed = tile(name, PASS, F32, 4 * PASS, host, at)
+            picked = held[window][:].indirect(entries(PASS * g, PASS * (g + 1)))
             if engine == "S":
-                nc.scalar.activation(held["xl", j, g0][:], held["xr", j][:].indirect(entries), COPY)
+                nc.scalar.activation(listed[:], picked, COPY)
+                held[name, "places"] = [listed[:, t:PASS:4] for t in range(4)]
             else:
-                nc.vector.tensor_copy(held["xl", j, g0][:], window["x%d" % j][:].indirect(entries))
+                nc.vector.tensor_copy(listed[:].rearrange("p (t s) -> p s t", t=4), picked)
+                held[name, "places"] = [listed[:, P * t : P * (t + 1)] for t in range(4)]
 
-        def turn_x(j, g0, g1, bank=None):
-            turn_words(("xb", j, g0), held["xl", j, g0], g0, g1, bank)
+        def gather_shared(window, g, cut):
+            name = "%s_listed%d" % (window, g)
+            listed = tile(name, PASS, F32, 4 * PASS)
+            nc.vector.tensor_copy(listed[:, 0:cut], held[window][:].indirect(entries(PASS * g, PASS * g + cut)))
+            nc.scalar.activation(listed[:, cut:PASS], held[window][:].indirect(entries(PASS * g + cut, PASS * (g + 1))), COPY)
+            held[name, "places"] = [listed[:, t:PASS:4] for t in range(4)]
 
-        def stage_x(j, g, engine="S"):
-            if ("xs", j) not in held:
-                held["xs", j] = tile("xs%d" % j, [P, N], BF16, "a%d" % j)
-            target = held["xs", j][:, PASS * g : PASS * (g + 1)].bitcast(F32).rearrange("p (d u) -> p d u", u=2)
-            evacuate(engine, target, held["xb", j, g][:, 0].rearrange("p u d -> p d u"))
+        def turn_f32(window, g, bank):
+            turned = bank_tile("%s_turned%d" % (window, g), bank)
+            for t in range(4):
+                nc.tensor.transpose(turned[:, P * t : P * (t + 1)], held["%s_listed%d" % (window, g), "places"][t], eye[:])
+
+        def pick_ts(g, engine="V"):
+            copy(engine, ts_cols[:, 4 * g : 4 * (g + 1)], held["ts_window_turned%d" % g][:, P - 1 : PASS : P])
+
+        def weigh(j, g, host=None, at=0):
+            staged = tile("z_staged%d%d" % (j, g), PASS, BF16, 2 * PASS, host, at)
+            nc.vector.tensor_tensor(
+                staged[:].rearrange("p (n t) -> p n t", t=4),
+                held["y%d_turned%d" % (j, g)][:].rearrange("p (t n) -> p n t", t=4),
+                ts_cols[:, 4 * g : 4 * (g + 1)].unsqueeze(1).to_broadcast([P, P, 4]),
+                MULT,
+            )
+
+        def quantize_dz(j, g):
+            nc.vector.quantize_mx(
+                out=z_codes[g][:, P * j : P * (j + 1)].bitcast(E5M2),
+                scales=z_scales[g][:, P * j : P * (j + 1)],
+                in_=held["z_staged%d%d" % (j, g)][:],
+            )
+
+        def gather_x(j, s0, s1, engine, host=None, at=0):
+            g = s0 // PASS
+            name = "x_listed%d%d" % (j, g)
+            if name not in held:
+                tile(name, PASS, BF16, 4 * PASS, host, at)
+            target = held[name][:, s0 - PASS * g : s1 - PASS * g]
+            picked = held["x%d" % j][:].indirect(entries(s0, s1))
+            if engine == "S":
+                nc.scalar.activation(target, picked, COPY)
+            else:
+                nc.vector.tensor_copy(target, picked)
+
+        def turn_x(j, g, bank):
+            turned = bank_tile("x_turned%d%d" % (j, g), bank)
+            words = held["x_listed%d%d" % (j, g)][:].bitcast(F32)
+            for u in range(2):
+                nc.tensor.transpose(turned[:, P * u : P * (u + 1)], words[:, u : 2 * P : 2], eye[:])
+
+        def stage_x(j, g, engine="S", host=None, at=0, passes=1):
+            name = "x_staged%d%d" % (j, g - g % passes)
+            if name not in held:
+                tile(name, PASS * passes, BF16, 2 * PASS * passes, host, at)
+            target = held[name][:, PASS * (g % passes) : PASS * (g % passes + 1)].bitcast(F32).rearrange("p (d u) -> p d u", u=2)
+            copy(engine, target, held["x_turned%d%d" % (j, g)][:, 0 : 2 * P].rearrange("p (u d) -> p d u", u=2))
 
         def quantize_x(j, g0, g1, host=None, at=0):
-            codes = tile("xc%d%d" % (j, g0), [P, P * (g1 - g0)], U32, host, at)
+            codes = tile("x_codes%d%d" % (j, g0), P * (g1 - g0), U32, 4 * P * (g1 - g0), host, at)
             for g in range(g0, g1):
-                held["xc", j, g] = codes[:, (g - g0) * P : (g - g0 + 1) * P]
+                held["x_codes", j, g] = codes[:, (g - g0) * P : (g - g0 + 1) * P]
             nc.vector.quantize_mx(
-                out=codes[:].bitcast(E4M3), scales=x_scales[j][:, g0 * P : g1 * P], in_=held["xs", j][:, PASS * g0 : PASS * g1]
+                out=codes[:].bitcast(E4M3),
+                scales=x_scales[j][:, g0 * P : g1 * P],
+                in_=held["x_staged%d%d" % (j, g0)][:],
             )
 
-        def multiply(j, h, g, bank=None):
-            if g == 0:
-                held["acc", j, h] = bank_tile([P, PASS], bank)
+        def multiply(j, n0, n1, g, sums, at=0):
             nc.tensor.matmul_mx(
-                out=held["acc", j, h][:],
-                lhsT=held["xc", j, g].bitcast(E4M3),
+                out=held[sums][:, at : at + n1 - n0],
+                lhsT=held["x_codes", j, g].bitcast(E4M3),
                 lhsT_scale=x_scales[j][:, g * P : (g + 1) * P],
-                rhs=held["zc", h, g][:].bitcast(E5M2),
-                rhs_scale=z_scales[h][:, PASS * g : PASS * (g + 1)],
+                rhs=z_codes[g][:, n0:n1].bitcast(E5M2),
+                rhs_scale=z_scales[g][:, n0:n1],
                 start=(g == 0),
                 stop=(g == 1),
             )
 
-        def put_out(j, h, engine, parts=1, host=None, at=0):
-            result = tile("out%d%d" % (j, h), [P, PASS], F32, host, at)
-            for k in range(parts):
-                cols = slice(k * PASS // parts, (k + 1) * PASS // parts)
-                evacuate(engine, result[:, cols], held["acc", j, h][:, cols])
-                nc.sync.dma_start(out[0, j * P : (j + 1) * P, h * PASS + cols.start : h * PASS + cols.stop], result[:, cols])
+        def product(j, n0, n1, sums, at=0):
+            for g in range(2):
+                multiply(j, n0, n1, g, sums, at)
 
-        def dy_back(j, banks):
-            for g in range(2):
-                turn_dz32(j, g, banks[g])
-                stage_dz32(j, g)
+        def put_out(sums, c0, c1, rows, n0, engine, host=None, at=0):
+            width = (c1 - c0) // len(rows)
+            result = tile("%s_out%d" % (sums, c0), c1 - c0, F32, 4 * (c1 - c0), host, at)
+            copy(engine, result[:], held[sums][:, c0:c1])
+            target = out[0, rows[0] * P : (rows[-1] + 1) * P, n0 : n0 + width].rearrange("(j p) n -> p j n", p=P)
+            nc.sync.dma_start(target, result[:].rearrange("p (j n) -> p j n", n=width))
 
-        def x_on_scalar(j):
-            round_x(j, 0, 1)
+        def dy(j, engines, banks):
             for g in range(2):
-                gather_x(j, g, g + 1, "V" if (j, g) == (0, 0) else "S")
+                gather_f32("y%d" % j, g, engines[g])
             for g in range(2):
-                turn_x(j, g, g + 1, 6 + g)
-                stage_x(j, g)
+                turn_f32("y%d" % j, g, banks[g])
+
+        def finish_dz(j, host=None):
+            for g in range(2):
+                weigh(j, g, host, 1024 * g)
+            for g in range(2):
+                quantize_dz(j, g)
+
+        def take_x(j, engines, banks):
+            for g in range(2):
+                gather_x(j, PASS * g, PASS * (g + 1), engines[g])
+            for g in range(2):
+                turn_x(j, g, banks[g])
+
+        def products(rows, n0, n1, sums, bank):
+            bank_tile(sums, bank)
+            for k, j in enumerate(rows):
+                product(j, n0, n1, sums, (n1 - n0) * k)
 
         for g in range(2):
-            gather_ts(g)
-        for g in range(2):
-            spread_ts(g)
-        x_on_scalar(0)
-        for g in range(2):
-            gather_dz(0, g, g + 1)
-        quantize_x(0, 0, 2, "y0")
-        x_on_scalar(1)
-        dy_back(0, (6, 7))
-        for j in range(1, 4):
-            gather_dz(j, 0, 2)
-            dy_back(j, (0, 1) if j % 2 else (2, 3))
-        gather_dz(4, 0, 2)
-        quantize_x(1, 0, 2, "y4", 4096)
-        for g in range(2):
-            quantize_dz(0, g, 0, 4, "y4", 2048 * g)
-        for j in range(2):
+            gather_f32("ts_window", g, "V")
+            turn_f32("ts_window", g, g)
+            pick_ts(g)
+        for i in range(2):
+            take_x(i, "VS" if i == 0 else "SS", (4, 5))
             for g in range(2):
-                multiply(j, 0, g, 4 + j)
-        x_on_scalar(2)
-        dy_back(4, (6, 7))
-        for j in range(5, 7):
-            gather_dz(j, 0, 2)
-            dy_back(j, (0, 1) if j % 2 else (2, 3))
-        gather_dz(7, 0, 1)
-        gather_dz(7, 1, 2, "a5")
-        dy_back(7, (0, 1))
-        quantize_x(2, 0, 2, "y7")
-        for g in range(2):
-            quantize_dz(1, g, 0, 4, "y7", 2048 + 2048 * g)
-        for g in range(2):
-            multiply(2, 0, g, 2)
-        for g in range(2):
-            for j in range(3):
-                multiply(j, 1, g, (3, 0, 6)[j])
-        put_out(0, 0, "S", 1, "a5")
-        put_out(1, 0, "S", 1, "y7", 6144)
-        put_out(2, 0, "S")
-        for g in range(2):
-            gather_x(3, g, g + 1, "V")
-            turn_x(3, g, g + 1, (1, 7)[g])
-            stage_x(3, g)
-        quantize_x(3, 0, 1, "x3")
-        put_out(0, 1, "S")
-        put_out(1, 1, "V", 1, "x3", 2048)
-        put_out(2, 1, "V", 1, "x3", 4096)
-        quantize_x(3, 1, 2)
-        for g in range(2):
+                stage_x(i, g, passes=2)
+            dy(2 * i, "VV", (0, 1))
+            quantize_x(i, 0, 2, "y%d_listed0" % (2 * i))
+            finish_dz(2 * i)
+            if i == 1:
+                product(1, 0, 256, "q0", 256)
+            dy(2 * i + 1, "SS", (2, 3))
+            if i == 0:
+                finish_dz(1)
+                bank_tile("q0", 6)
+                product(0, 0, 256, "q0")
+        put_out("q0", 0, PASS, [0, 1], 0, "S", "y3_listed0")
+        dy(4, "VV", (0, 1))
+        finish_dz(3, "y4_listed0")
+        finish_dz(4)
+        dy(5, "SS", (2, 3))
+        finish_dz(5)
+        products([0, 1], 256, 512, "q1", 2)
+        dy(6, "SS", (0, 1))
+        dy(7, "VS", (4, 5))
+        put_out("q1", 0, PASS, [0, 1], 256, "S", "y7", 4096)
+        finish_dz(6, "y7")
+        products([0, 1], 512, 768, "q2", 0)
+        finish_dz(7)
+        products([0, 1], 768, DV, "q3", 4)
+        take_x(2, "SS", (6, 7))
+        stage_x(2, 0, "V")
+        take_x(3, "VS", (3, 1))
+        quantize_x(2, 0, 1, "x3")
+        stage_x(2, 1, "S", "x3", 1024)
+        quantize_x(2, 1, 2)
+        for j in range(2, 4):
+            if j == 3:
+                put_out("q2", 0, PASS, [0, 1], 512, "V", "x3", 4096)
+                for g in range(2):
+                    stage_x(3, g, "S")
+                    quantize_x(3, g, g + 1)
+                put_out("q3", 0, PASS, [0, 1], 768, "S", "x_listed31")
             for h in range(2):
-                multiply(3, h, g, 4 + h)
-        put_out(3, 0, "V", 2)
-        put_out(3, 1, "S", 2)
+                bank_tile("x%dh%d" % (j, h), ((6, 7), (5, 2))[j - 2][h])
+            for g in range(2):
+                for h in range(2):
+                    multiply(j, PASS * h, PASS * (h + 1), g, "x%dh%d" % (j, h))
+        for h in range(2):
+            put_out("x2h%d" % h, 0, PASS, [2], PASS * h, "VS"[h])
+        for c0 in (0, 256):
+            for h in range(2):
+                put_out("x3h%d" % h, c0, c0 + 256, [3], PASS * h + c0, "VS"[h])

@@ -220,12 +220,12 @@ def tile_attend_gex_w_kernel(tc, xT, dyT, ts, offs, out):
         dy(7, "VS", (4, 5))
         put_out("q1", 0, PASS, [0, 1], 256, "S", "y7", 4096)
         finish_dz(6, "y7")
-        products([0, 1], 512, 768, "q2", 0)
+        products([0, 1], 512, 768, "q2", 1)
         finish_dz(7)
         products([0, 1], 768, DV, "q3", 4)
         take_x(2, "SS", (6, 7))
         stage_x(2, 0, "V")
-        take_x(3, "VS", (3, 1))
+        take_x(3, "VS", (3, 0))
         quantize_x(2, 0, 1, "x3")
         stage_x(2, 1, "S", "x3", 1024)
         quantize_x(2, 1, 2)

@@ -18,6 +18,10 @@ MULT = mybir.AluOpType.mult
 
 P = 128
 PASS = 512
+PLACES = 4
+QUARTER = DV // 4
+BANK_BYTES = 4 * PASS
+VECTOR, SCALAR = "vector", "scalar"
 ARRIVAL = ["x0", "y0", "y1", "x1", "y2", "y3", "y4", "y5", "y6", "y7", "x2", "x3"]
 
 
@@ -28,25 +32,27 @@ def tile_attend_gex_w_kernel(tc, xT, dyT, ts, offs, out):
         arena = ctx.enter_context(tc.tile_pool(name="arena", bufs=1))
         psum = ctx.enter_context(tc.psum_pool(name="psum", bufs=1))
         place = {"end": 0}
-        held = {}
+        tiles = {}
+        by_place = {}
+        x_codes = {}
 
-        def tile(name, columns, dtype, nbytes, host=None, at=0):
-            if host is None:
+        def tile(name, columns, dtype, nbytes, over=None, at=0):
+            if over is None:
                 place[name] = place["end"]
                 place["end"] = place["end"] + nbytes
             else:
-                place[name] = place[host] + at
-            held[name] = arena.tile([P, columns], dtype, name=name, align_bytes=64, offset=place[name])
-            return held[name]
+                place[name] = place[over] + at
+            tiles[name] = arena.tile([P, columns], dtype, name=name, align_bytes=64, offset=place[name])
+            return tiles[name]
 
         def bank_tile(name, bank):
-            held[name] = psum.tile([P, PASS], F32, name=name, offset=2048 * bank)
-            return held[name]
+            tiles[name] = psum.tile([P, PASS], F32, name=name, offset=BANK_BYTES * bank)
+            return tiles[name]
 
         offsets = keep.tile([P, N // 16], U16, name="offsets")
         eye = tile("eye", P, F32, 4 * P)
-        ts_window = tile("ts_window", T, F32, 4 * T)
-        ts_cols = tile("ts_cols", 8, F32, 64)
+        ts_window = tile("ts", T, F32, 4 * T)
+        ts_slots = tile("ts_slots", 2 * PLACES, F32, 64)
         z_codes = [tile("z_codes%d" % g, DV, U32, 4 * DV) for g in range(2)]
         z_scales = [tile("z_scales%d" % g, DV, U8, DV) for g in range(2)]
         x_scales = [tile("x_scales%d" % j, 2 * P, U8, 2 * P) for j in range(4)]
@@ -60,47 +66,41 @@ def tile_attend_gex_w_kernel(tc, xT, dyT, ts, offs, out):
             nc.sync.dma_start(tile(name, T, F32, 4 * T)[:], source[j * P : (j + 1) * P, :])
         make_identity(nc, eye[:])
 
-        def entries(s0, s1):
-            return offsets[:, s0 // 16 : s1 // 16]
+        def listed_columns(window, g):
+            return tiles[window][:].indirect(offsets[:, PASS * g // 16 : PASS * (g + 1) // 16])
 
         def copy(engine, target, source):
-            if engine == "S":
+            if engine == SCALAR:
                 nc.scalar.copy(target, source)
             else:
                 nc.vector.tensor_copy(target, source)
 
-        def gather_f32(window, g, engine, host=None, at=0):
-            name = "%s_listed%d" % (window, g)
-            listed = tile(name, PASS, F32, 4 * PASS, host, at)
-            picked = held[window][:].indirect(entries(PASS * g, PASS * (g + 1)))
-            if engine == "S":
-                nc.scalar.activation(listed[:], picked, COPY)
-                held[name, "places"] = [listed[:, t:PASS:4] for t in range(4)]
+        def gather_f32(window, g, engine):
+            listed = tile("%s_listed%d" % (window, g), PASS, F32, 4 * PASS)
+            if engine == SCALAR:
+                nc.scalar.activation(listed[:], listed_columns(window, g), COPY)
+                by_place[window, g] = [listed[:, t:PASS:PLACES] for t in range(PLACES)]
             else:
-                nc.vector.tensor_copy(listed[:].rearrange("p (t s) -> p s t", t=4), picked)
-                held[name, "places"] = [listed[:, P * t : P * (t + 1)] for t in range(4)]
-
-        def gather_shared(window, g, cut):
-            name = "%s_listed%d" % (window, g)
-            listed = tile(name, PASS, F32, 4 * PASS)
-            nc.vector.tensor_copy(listed[:, 0:cut], held[window][:].indirect(entries(PASS * g, PASS * g + cut)))
-            nc.scalar.activation(listed[:, cut:PASS], held[window][:].indirect(entries(PASS * g + cut, PASS * (g + 1))), COPY)
-            held[name, "places"] = [listed[:, t:PASS:4] for t in range(4)]
+                nc.vector.tensor_copy(listed[:].rearrange("p (t s) -> p s t", t=PLACES), listed_columns(window, g))
+                by_place[window, g] = [listed[:, P * t : P * (t + 1)] for t in range(PLACES)]
 
         def turn_f32(window, g, bank):
             turned = bank_tile("%s_turned%d" % (window, g), bank)
-            for t in range(4):
-                nc.tensor.transpose(turned[:, P * t : P * (t + 1)], held["%s_listed%d" % (window, g), "places"][t], eye[:])
+            for t in range(PLACES):
+                nc.tensor.transpose(turned[:, P * t : P * (t + 1)], by_place[window, g][t], eye[:])
 
-        def pick_ts(g, engine="V"):
-            copy(engine, ts_cols[:, 4 * g : 4 * (g + 1)], held["ts_window_turned%d" % g][:, P - 1 : PASS : P])
+        def take_dy(j, engines, banks):
+            for g in range(2):
+                gather_f32("y%d" % j, g, engines[g])
+            for g in range(2):
+                turn_f32("y%d" % j, g, banks[g])
 
-        def weigh(j, g, host=None, at=0):
-            staged = tile("z_staged%d%d" % (j, g), PASS, BF16, 2 * PASS, host, at)
+        def weigh(j, g, over=None):
+            staged = tile("z_staged%d%d" % (j, g), PASS, BF16, 2 * PASS, over, 2 * PASS * g)
             nc.vector.tensor_tensor(
-                staged[:].rearrange("p (n t) -> p n t", t=4),
-                held["y%d_turned%d" % (j, g)][:].rearrange("p (t n) -> p n t", t=4),
-                ts_cols[:, 4 * g : 4 * (g + 1)].unsqueeze(1).to_broadcast([P, P, 4]),
+                staged[:].rearrange("p (n t) -> p n t", t=PLACES),
+                tiles["y%d_turned%d" % (j, g)][:].rearrange("p (t n) -> p n t", t=PLACES),
+                ts_slots[:, PLACES * g : PLACES * (g + 1)].unsqueeze(1).to_broadcast([P, P, PLACES]),
                 MULT,
             )
 
@@ -108,48 +108,49 @@ def tile_attend_gex_w_kernel(tc, xT, dyT, ts, offs, out):
             nc.vector.quantize_mx(
                 out=z_codes[g][:, P * j : P * (j + 1)].bitcast(E5M2),
                 scales=z_scales[g][:, P * j : P * (j + 1)],
-                in_=held["z_staged%d%d" % (j, g)][:],
+                in_=tiles["z_staged%d%d" % (j, g)][:],
             )
 
-        def gather_x(j, s0, s1, engine, host=None, at=0):
-            g = s0 // PASS
-            name = "x_listed%d%d" % (j, g)
-            if name not in held:
-                tile(name, PASS, BF16, 4 * PASS, host, at)
-            target = held[name][:, s0 - PASS * g : s1 - PASS * g]
-            picked = held["x%d" % j][:].indirect(entries(s0, s1))
-            if engine == "S":
-                nc.scalar.activation(target, picked, COPY)
-            else:
-                nc.vector.tensor_copy(target, picked)
+        def finish_dz(j, over=None):
+            for g in range(2):
+                weigh(j, g, over)
+            for g in range(2):
+                quantize_dz(j, g)
 
-        def turn_x(j, g, bank):
-            turned = bank_tile("x_turned%d%d" % (j, g), bank)
-            words = held["x_listed%d%d" % (j, g)][:].bitcast(F32)
-            for u in range(2):
-                nc.tensor.transpose(turned[:, P * u : P * (u + 1)], words[:, u : 2 * P : 2], eye[:])
+        def take_x(j, engines, banks):
+            for g in range(2):
+                listed = tile("x_listed%d%d" % (j, g), PASS, BF16, BANK_BYTES)
+                if engines[g] == SCALAR:
+                    nc.scalar.activation(listed[:], listed_columns("x%d" % j, g), COPY)
+                else:
+                    nc.vector.tensor_copy(listed[:], listed_columns("x%d" % j, g))
+            for g in range(2):
+                turned = bank_tile("x_turned%d%d" % (j, g), banks[g])
+                words = tiles["x_listed%d%d" % (j, g)][:].bitcast(F32)
+                for u in range(2):
+                    nc.tensor.transpose(turned[:, P * u : P * (u + 1)], words[:, u : 2 * P : 2], eye[:])
 
-        def stage_x(j, g, engine="S", host=None, at=0, passes=1):
-            name = "x_staged%d%d" % (j, g - g % passes)
-            if name not in held:
-                tile(name, PASS * passes, BF16, 2 * PASS * passes, host, at)
-            target = held[name][:, PASS * (g % passes) : PASS * (g % passes + 1)].bitcast(F32).rearrange("p (d u) -> p d u", u=2)
-            copy(engine, target, held["x_turned%d%d" % (j, g)][:, 0 : 2 * P].rearrange("p (u d) -> p d u", u=2))
+        def stage_x(j, g, engine, target):
+            source = tiles["x_turned%d%d" % (j, g)][:, 0 : 2 * P].rearrange("p (u d) -> p d u", u=2)
+            copy(engine, target.bitcast(F32).rearrange("p (d u) -> p d u", u=2), source)
 
-        def quantize_x(j, g0, g1, host=None, at=0):
-            codes = tile("x_codes%d%d" % (j, g0), P * (g1 - g0), U32, 4 * P * (g1 - g0), host, at)
+        def stage_x_pass(j, g, engine, over=None, at=0):
+            stage_x(j, g, engine, tile("x_staged%d%d" % (j, g), PASS, BF16, 2 * PASS, over, at)[:])
+
+        def quantize_x(j, g0, g1, over=None):
+            codes = tile("x_codes%d%d" % (j, g0), P * (g1 - g0), U32, 4 * P * (g1 - g0), over)
             for g in range(g0, g1):
-                held["x_codes", j, g] = codes[:, (g - g0) * P : (g - g0 + 1) * P]
+                x_codes[j, g] = codes[:, (g - g0) * P : (g - g0 + 1) * P]
             nc.vector.quantize_mx(
                 out=codes[:].bitcast(E4M3),
                 scales=x_scales[j][:, g0 * P : g1 * P],
-                in_=held["x_staged%d%d" % (j, g0)][:],
+                in_=tiles["x_staged%d%d" % (j, g0)][:],
             )
 
         def multiply(j, n0, n1, g, sums, at=0):
             nc.tensor.matmul_mx(
-                out=held[sums][:, at : at + n1 - n0],
-                lhsT=held["x_codes", j, g].bitcast(E4M3),
+                out=tiles[sums][:, at : at + n1 - n0],
+                lhsT=x_codes[j, g].bitcast(E4M3),
                 lhsT_scale=x_scales[j][:, g * P : (g + 1) * P],
                 rhs=z_codes[g][:, n0:n1].bitcast(E5M2),
                 rhs_scale=z_scales[g][:, n0:n1],
@@ -157,92 +158,89 @@ def tile_attend_gex_w_kernel(tc, xT, dyT, ts, offs, out):
                 stop=(g == 1),
             )
 
-        def product(j, n0, n1, sums, at=0):
+        def multiply_quarter(j, q):
             for g in range(2):
-                multiply(j, n0, n1, g, sums, at)
+                multiply(j, QUARTER * q, QUARTER * (q + 1), g, "quarter%d" % q, QUARTER * j)
 
-        def put_out(sums, c0, c1, rows, n0, engine, host=None, at=0):
+        def multiply_early(q, bank):
+            bank_tile("quarter%d" % q, bank)
+            for j in range(2):
+                multiply_quarter(j, q)
+
+        def put_out(sums, c0, c1, rows, n0, engine, over=None, at=0):
             width = (c1 - c0) // len(rows)
-            result = tile("%s_out%d" % (sums, c0), c1 - c0, F32, 4 * (c1 - c0), host, at)
-            copy(engine, result[:], held[sums][:, c0:c1])
+            result = tile("%s_out%d" % (sums, c0), c1 - c0, F32, 4 * (c1 - c0), over, at)
+            copy(engine, result[:], tiles[sums][:, c0:c1])
             target = out[0, rows[0] * P : (rows[-1] + 1) * P, n0 : n0 + width].rearrange("(j p) n -> p j n", p=P)
             nc.sync.dma_start(target, result[:].rearrange("p (j n) -> p j n", n=width))
 
-        def dy(j, engines, banks):
-            for g in range(2):
-                gather_f32("y%d" % j, g, engines[g])
-            for g in range(2):
-                turn_f32("y%d" % j, g, banks[g])
-
-        def finish_dz(j, host=None):
-            for g in range(2):
-                weigh(j, g, host, 1024 * g)
-            for g in range(2):
-                quantize_dz(j, g)
-
-        def take_x(j, engines, banks):
-            for g in range(2):
-                gather_x(j, PASS * g, PASS * (g + 1), engines[g])
-            for g in range(2):
-                turn_x(j, g, banks[g])
-
-        def products(rows, n0, n1, sums, bank):
-            bank_tile(sums, bank)
-            for k, j in enumerate(rows):
-                product(j, n0, n1, sums, (n1 - n0) * k)
+        def put_quarter(q, engine, over, at=0):
+            put_out("quarter%d" % q, 0, PASS, [0, 1], QUARTER * q, engine, over, at)
 
         for g in range(2):
-            gather_f32("ts_window", g, "V")
-            turn_f32("ts_window", g, g)
-            pick_ts(g)
-        for i in range(2):
-            take_x(i, "VS" if i == 0 else "SS", (4, 5))
+            gather_f32("ts", g, VECTOR)
+            turn_f32("ts", g, g)
+            nc.vector.tensor_copy(ts_slots[:, PLACES * g : PLACES * (g + 1)], tiles["ts_turned%d" % g][:, P - 1 : PASS : P])
+
+        for j in range(2):
+            take_x(j, (SCALAR if j else VECTOR, SCALAR), (4, 5))
+            staged = tile("x_staged%d0" % j, N, BF16, 2 * N)
             for g in range(2):
-                stage_x(i, g, passes=2)
-            dy(2 * i, "VV", (0, 1))
-            quantize_x(i, 0, 2, "y%d_listed0" % (2 * i))
-            finish_dz(2 * i)
-            if i == 1:
-                product(1, 0, 256, "q0", 256)
-            dy(2 * i + 1, "SS", (2, 3))
-            if i == 0:
+                stage_x(j, g, SCALAR, staged[:, PASS * g : PASS * (g + 1)])
+            take_dy(2 * j, (VECTOR, VECTOR), (0, 1))
+            quantize_x(j, 0, 2, over="y%d_listed0" % (2 * j))
+            finish_dz(2 * j)
+            if j:
+                multiply_quarter(1, 0)
+            take_dy(2 * j + 1, (SCALAR, SCALAR), (2, 3))
+            if not j:
                 finish_dz(1)
-                bank_tile("q0", 6)
-                product(0, 0, 256, "q0")
-        put_out("q0", 0, PASS, [0, 1], 0, "S", "y3_listed0")
-        dy(4, "VV", (0, 1))
-        finish_dz(3, "y4_listed0")
+                bank_tile("quarter0", 6)
+                multiply_quarter(0, 0)
+        put_quarter(0, SCALAR, over="y3_listed0")
+
+        take_dy(4, (VECTOR, VECTOR), (0, 1))
+        finish_dz(3, over="y4_listed0")
         finish_dz(4)
-        dy(5, "SS", (2, 3))
+        take_dy(5, (SCALAR, SCALAR), (2, 3))
         finish_dz(5)
-        products([0, 1], 256, 512, "q1", 2)
-        dy(6, "SS", (0, 1))
-        dy(7, "VS", (4, 5))
-        put_out("q1", 0, PASS, [0, 1], 256, "S", "y7", 4096)
-        finish_dz(6, "y7")
-        products([0, 1], 512, 768, "q2", 1)
-        finish_dz(7)
-        products([0, 1], 768, DV, "q3", 4)
-        take_x(2, "SS", (6, 7))
-        stage_x(2, 0, "V")
-        take_x(3, "VS", (3, 0))
-        quantize_x(2, 0, 1, "x3")
-        stage_x(2, 1, "S", "x3", 1024)
+        multiply_early(1, 2)
+        take_dy(6, (SCALAR, SCALAR), (0, 1))
+        take_dy(7, (VECTOR, SCALAR), (4, 5))
+        put_quarter(1, SCALAR, over="y7", at=2 * BANK_BYTES)
+        for g in range(2):
+            weigh(6, g, over="y7")
+        multiply_early(2, 0)
+        for g in range(2):
+            weigh(7, g)
+        for j in (6, 7):
+            for g in range(2):
+                quantize_dz(j, g)
+        multiply_early(3, 4)
+
+        take_x(2, (SCALAR, SCALAR), (6, 7))
+        stage_x_pass(2, 0, VECTOR)
+        take_x(3, (VECTOR, SCALAR), (3, 1))
+        quantize_x(2, 0, 1, over="x3")
+        stage_x_pass(2, 1, SCALAR, over="x3", at=2 * PASS)
         quantize_x(2, 1, 2)
-        for j in range(2, 4):
-            if j == 3:
-                put_out("q2", 0, PASS, [0, 1], 512, "V", "x3", 4096)
-                for g in range(2):
-                    stage_x(3, g, "S")
-                    quantize_x(3, g, g + 1)
-                put_out("q3", 0, PASS, [0, 1], 768, "S", "x_listed31")
+
+        def multiply_late(j, banks):
             for h in range(2):
-                bank_tile("x%dh%d" % (j, h), ((6, 7), (5, 2))[j - 2][h])
+                bank_tile("x%d_half%d" % (j, h), banks[h])
             for g in range(2):
                 for h in range(2):
-                    multiply(j, PASS * h, PASS * (h + 1), g, "x%dh%d" % (j, h))
+                    multiply(j, PASS * h, PASS * (h + 1), g, "x%d_half%d" % (j, h))
+
+        multiply_late(2, (6, 7))
+        put_quarter(2, VECTOR, over="x3", at=2 * BANK_BYTES)
+        for g in range(2):
+            stage_x_pass(3, g, SCALAR)
+            quantize_x(3, g, g + 1)
+        put_quarter(3, SCALAR, over="x_listed31")
+        multiply_late(3, (5, 2))
         for h in range(2):
-            put_out("x2h%d" % h, 0, PASS, [2], PASS * h, "VS"[h])
-        for c0 in (0, 256):
+            put_out("x2_half%d" % h, 0, PASS, [2], PASS * h, (VECTOR, SCALAR)[h])
+        for c0 in (0, QUARTER):
             for h in range(2):
-                put_out("x3h%d" % h, c0, c0 + 256, [3], PASS * h + c0, "VS"[h])
+                put_out("x3_half%d" % h, c0, c0 + QUARTER, [3], PASS * h + c0, (VECTOR, SCALAR)[h])

@@ -22,6 +22,7 @@ PLACES = 4
 QUARTER = DV // 4
 BANK_BYTES = 4 * PASS
 VECTOR, SCALAR = "vector", "scalar"
+Y4_ON_VECTOR = 192
 ARRIVAL = ["x0", "y0", "y1", "x1", "y2", "y3", "y4", "y5", "y6", "y7", "x2", "x3"]
 
 
@@ -66,8 +67,8 @@ def tile_attend_gex_w_kernel(tc, xT, dyT, ts, offs, out):
             nc.sync.dma_start(tile(name, T, F32, 4 * T)[:], source[j * P : (j + 1) * P, :])
         make_identity(nc, eye[:])
 
-        def listed_columns(window, g):
-            return tiles[window][:].indirect(offsets[:, PASS * g // 16 : PASS * (g + 1) // 16])
+        def listed_columns(window, g, s0=0, s1=PASS):
+            return tiles[window][:].indirect(offsets[:, (PASS * g + s0) // 16 : (PASS * g + s1) // 16])
 
         def copy(engine, target, source):
             if engine == SCALAR:
@@ -83,6 +84,12 @@ def tile_attend_gex_w_kernel(tc, xT, dyT, ts, offs, out):
             else:
                 nc.vector.tensor_copy(listed[:].rearrange("p (t s) -> p s t", t=PLACES), listed_columns(window, g))
                 by_place[window, g] = [listed[:, P * t : P * (t + 1)] for t in range(PLACES)]
+
+        def gather_shared(window, g, cut):
+            listed = tile("%s_listed%d" % (window, g), PASS, F32, 4 * PASS)
+            nc.vector.tensor_copy(listed[:, 0:cut], listed_columns(window, g, 0, cut))
+            nc.scalar.activation(listed[:, cut:PASS], listed_columns(window, g, cut, PASS), COPY)
+            by_place[window, g] = [listed[:, t:PASS:PLACES] for t in range(PLACES)]
 
         def turn_f32(window, g, bank):
             turned = bank_tile("%s_turned%d" % (window, g), bank)
@@ -111,11 +118,15 @@ def tile_attend_gex_w_kernel(tc, xT, dyT, ts, offs, out):
                 in_=tiles["z_staged%d%d" % (j, g)][:],
             )
 
-        def finish_dz(j, over=None):
+        def quantize_windows(*windows):
+            for j in windows:
+                for g in range(2):
+                    quantize_dz(j, g)
+
+        def finish_dz(j):
             for g in range(2):
-                weigh(j, g, over)
-            for g in range(2):
-                quantize_dz(j, g)
+                weigh(j, g)
+            quantize_windows(j)
 
         def take_x(j, engines, banks):
             for g in range(2):
@@ -199,9 +210,15 @@ def tile_attend_gex_w_kernel(tc, xT, dyT, ts, offs, out):
                 multiply_quarter(0, 0)
         put_quarter(0, SCALAR, over="y3_listed0")
 
-        take_dy(4, (VECTOR, VECTOR), (0, 1))
-        finish_dz(3, over="y4_listed0")
-        finish_dz(4)
+        gather_f32("y4", 0, VECTOR)
+        gather_shared("y4", 1, Y4_ON_VECTOR)
+        for g in range(2):
+            turn_f32("y4", g, g)
+        for g in range(2):
+            weigh(3, g, over="y4_listed0")
+        for g in range(2):
+            weigh(4, g)
+        quantize_windows(3, 4)
         take_dy(5, (SCALAR, SCALAR), (2, 3))
         finish_dz(5)
         multiply_early(1, 2)
@@ -213,9 +230,7 @@ def tile_attend_gex_w_kernel(tc, xT, dyT, ts, offs, out):
         multiply_early(2, 0)
         for g in range(2):
             weigh(7, g)
-        for j in (6, 7):
-            for g in range(2):
-                quantize_dz(j, g)
+        quantize_windows(6, 7)
         multiply_early(3, 4)
 
         take_x(2, (SCALAR, SCALAR), (6, 7))

from contextlib import ExitStack

import concourse.mybir as mybir
from concourse.masks import make_identity

N, T, D, DV = 1024, 2048, 512, 1024
FLOPS = 2 * N * D * DV

F32 = mybir.dt.float32
BF16 = mybir.dt.bfloat16
U32 = mybir.dt.uint32
U16 = mybir.dt.uint16
U8 = mybir.dt.uint8
E4M3 = mybir.dt.float8_e4m3fn_x4
E5M2 = mybir.dt.float8_e5m2_x4
COPY = mybir.ActivationFunctionType.Copy
MULT = mybir.AluOpType.mult

P = 128
PASS = 512
PLACES = 4
QUARTER = DV // 4
BANK_BYTES = 4 * PASS
VECTOR, SCALAR = "vector", "scalar"
Y4_ON_VECTOR = 192
ARRIVAL = ["x0", "y0", "y1", "x1", "y2", "y3", "y4", "y5", "y6", "y7", "x2", "x3"]


def tile_attend_gex_w_kernel(tc, xT, dyT, ts, offs, out):
    nc = tc.nc
    with ExitStack() as ctx:
        keep = ctx.enter_context(tc.tile_pool(name="keep", bufs=1))
        arena = ctx.enter_context(tc.tile_pool(name="arena", bufs=1))
        psum = ctx.enter_context(tc.psum_pool(name="psum", bufs=1))
        place = {"end": 0}
        tiles = {}
        by_place = {}
        x_codes = {}

        def tile(name, columns, dtype, nbytes, over=None, at=0):
            if over is None:
                place[name] = place["end"]
                place["end"] = place["end"] + nbytes
            else:
                place[name] = place[over] + at
            tiles[name] = arena.tile([P, columns], dtype, name=name, align_bytes=64, offset=place[name])
            return tiles[name]

        def bank_tile(name, bank):
            tiles[name] = psum.tile([P, PASS], F32, name=name, offset=BANK_BYTES * bank)
            return tiles[name]

        offsets = keep.tile([P, N // 16], U16, name="offsets")
        eye = tile("eye", P, F32, 4 * P)
        ts_window = tile("ts", T, F32, 4 * T)
        ts_slots = tile("ts_slots", 2 * PLACES, F32, 64)
        z_codes = [tile("z_codes%d" % g, DV, U32, 4 * DV) for g in range(2)]
        z_scales = [tile("z_scales%d" % g, DV, U8, DV) for g in range(2)]
        x_scales = [tile("x_scales%d" % j, 2 * P, U8, 2 * P) for j in range(4)]

        nc.vector.memset(ts_window[0 : P - 1, :], 0.0)
        nc.sync.dma_start(offsets[:], offs)
        nc.scalar.dma_start(ts_window[P - 1 : P, :], ts[0:1, :])
        for name in ARRIVAL:
            j = int(name[1])
            source = xT if name[0] == "x" else dyT
            nc.sync.dma_start(tile(name, T, F32, 4 * T)[:], source[j * P : (j + 1) * P, :])
        make_identity(nc, eye[:])

        def listed_columns(window, g, s0=0, s1=PASS):
            return tiles[window][:].indirect(offsets[:, (PASS * g + s0) // 16 : (PASS * g + s1) // 16])

        def copy(engine, target, source):
            if engine == SCALAR:
                nc.scalar.copy(target, source)
            else:
                nc.vector.tensor_copy(target, source)

        def gather_f32(window, g, engine):
            listed = tile("%s_listed%d" % (window, g), PASS, F32, 4 * PASS)
            if engine == SCALAR:
                nc.scalar.activation(listed[:], listed_columns(window, g), COPY)
                by_place[window, g] = [listed[:, t:PASS:PLACES] for t in range(PLACES)]
            else:
                nc.vector.tensor_copy(listed[:].rearrange("p (t s) -> p s t", t=PLACES), listed_columns(window, g))
                by_place[window, g] = [listed[:, P * t : P * (t + 1)] for t in range(PLACES)]

        def gather_shared(window, g, cut):
            listed = tile("%s_listed%d" % (window, g), PASS, F32, 4 * PASS)
            nc.vector.tensor_copy(listed[:, 0:cut], listed_columns(window, g, 0, cut))
            nc.scalar.activation(listed[:, cut:PASS], listed_columns(window, g, cut, PASS), COPY)
            by_place[window, g] = [listed[:, t:PASS:PLACES] for t in range(PLACES)]

        def turn_f32(window, g, bank):
            turned = bank_tile("%s_turned%d" % (window, g), bank)
            for t in range(PLACES):
                nc.tensor.transpose(turned[:, P * t : P * (t + 1)], by_place[window, g][t], eye[:])

        def take_dy(j, engines, banks):
            for g in range(2):
                gather_f32("y%d" % j, g, engines[g])
            for g in range(2):
                turn_f32("y%d" % j, g, banks[g])

        def weigh(j, g, over=None):
            staged = tile("z_staged%d%d" % (j, g), PASS, BF16, 2 * PASS, over, 2 * PASS * g)
            nc.vector.tensor_tensor(
                staged[:].rearrange("p (n t) -> p n t", t=PLACES),
                tiles["y%d_turned%d" % (j, g)][:].rearrange("p (t n) -> p n t", t=PLACES),
                ts_slots[:, PLACES * g : PLACES * (g + 1)].unsqueeze(1).to_broadcast([P, P, PLACES]),
                MULT,
            )

        def quantize_dz(j, g):
            nc.vector.quantize_mx(
                out=z_codes[g][:, P * j : P * (j + 1)].bitcast(E5M2),
                scales=z_scales[g][:, P * j : P * (j + 1)],
                in_=tiles["z_staged%d%d" % (j, g)][:],
            )

        def quantize_windows(*windows):
            for j in windows:
                for g in range(2):
                    quantize_dz(j, g)

        def finish_dz(j):
            for g in range(2):
                weigh(j, g)
            quantize_windows(j)

        def take_x(j, engines, banks):
            for g in range(2):
                listed = tile("x_listed%d%d" % (j, g), PASS, BF16, BANK_BYTES)
                if engines[g] == SCALAR:
                    nc.scalar.activation(listed[:], listed_columns("x%d" % j, g), COPY)
                else:
                    nc.vector.tensor_copy(listed[:], listed_columns("x%d" % j, g))
            for g in range(2):
                turned = bank_tile("x_turned%d%d" % (j, g), banks[g])
                words = tiles["x_listed%d%d" % (j, g)][:].bitcast(F32)
                for u in range(2):
                    nc.tensor.transpose(turned[:, P * u : P * (u + 1)], words[:, u : 2 * P : 2], eye[:])

        def stage_x(j, g, engine, target):
            source = tiles["x_turned%d%d" % (j, g)][:, 0 : 2 * P].rearrange("p (u d) -> p d u", u=2)
            copy(engine, target.bitcast(F32).rearrange("p (d u) -> p d u", u=2), source)

        def stage_x_pass(j, g, engine, over=None, at=0):
            stage_x(j, g, engine, tile("x_staged%d%d" % (j, g), PASS, BF16, 2 * PASS, over, at)[:])

        def quantize_x(j, g0, g1, over=None):
            codes = tile("x_codes%d%d" % (j, g0), P * (g1 - g0), U32, 4 * P * (g1 - g0), over)
            for g in range(g0, g1):
                x_codes[j, g] = codes[:, (g - g0) * P : (g - g0 + 1) * P]
            nc.vector.quantize_mx(
                out=codes[:].bitcast(E4M3),
                scales=x_scales[j][:, g0 * P : g1 * P],
                in_=tiles["x_staged%d%d" % (j, g0)][:],
            )

        def multiply(j, n0, n1, g, sums, at=0):
            nc.tensor.matmul_mx(
                out=tiles[sums][:, at : at + n1 - n0],
                lhsT=x_codes[j, g].bitcast(E4M3),
                lhsT_scale=x_scales[j][:, g * P : (g + 1) * P],
                rhs=z_codes[g][:, n0:n1].bitcast(E5M2),
                rhs_scale=z_scales[g][:, n0:n1],
                start=(g == 0),
                stop=(g == 1),
            )

        def multiply_quarter(j, q):
            for g in range(2):
                multiply(j, QUARTER * q, QUARTER * (q + 1), g, "quarter%d" % q, QUARTER * j)

        def multiply_early(q, bank):
            bank_tile("quarter%d" % q, bank)
            for j in range(2):
                multiply_quarter(j, q)

        def put_out(sums, c0, c1, rows, n0, engine, over=None, at=0):
            width = (c1 - c0) // len(rows)
            result = tile("%s_out%d" % (sums, c0), c1 - c0, F32, 4 * (c1 - c0), over, at)
            copy(engine, result[:], tiles[sums][:, c0:c1])
            target = out[0, rows[0] * P : (rows[-1] + 1) * P, n0 : n0 + width].rearrange("(j p) n -> p j n", p=P)
            nc.sync.dma_start(target, result[:].rearrange("p (j n) -> p j n", n=width))

        def put_quarter(q, engine, over, at=0):
            put_out("quarter%d" % q, 0, PASS, [0, 1], QUARTER * q, engine, over, at)

        for g in range(2):
            gather_f32("ts", g, VECTOR)
            turn_f32("ts", g, g)
            nc.vector.tensor_copy(ts_slots[:, PLACES * g : PLACES * (g + 1)], tiles["ts_turned%d" % g][:, P - 1 : PASS : P])

        for j in range(2):
            take_x(j, (SCALAR if j else VECTOR, SCALAR), (4, 5))
            staged = tile("x_staged%d0" % j, N, BF16, 2 * N)
            for g in range(2):
                stage_x(j, g, SCALAR, staged[:, PASS * g : PASS * (g + 1)])
            take_dy(2 * j, (VECTOR, VECTOR), (0, 1))
            quantize_x(j, 0, 2, over="y%d_listed0" % (2 * j))
            finish_dz(2 * j)
            if j:
                multiply_quarter(1, 0)
            take_dy(2 * j + 1, (SCALAR, SCALAR), (2, 3))
            if not j:
                finish_dz(1)
                bank_tile("quarter0", 6)
                multiply_quarter(0, 0)
        put_quarter(0, SCALAR, over="y3_listed0")

        gather_f32("y4", 0, VECTOR)
        gather_shared("y4", 1, Y4_ON_VECTOR)
        for g in range(2):
            turn_f32("y4", g, g)
        for g in range(2):
            weigh(3, g, over="y4_listed0")
        for g in range(2):
            weigh(4, g)
        quantize_windows(3, 4)
        take_dy(5, (SCALAR, SCALAR), (2, 3))
        finish_dz(5)
        multiply_early(1, 2)
        take_dy(6, (SCALAR, SCALAR), (0, 1))
        take_dy(7, (VECTOR, SCALAR), (4, 5))
        put_quarter(1, SCALAR, over="y7", at=2 * BANK_BYTES)
        for g in range(2):
            weigh(6, g, over="y7")
        multiply_early(2, 0)
        for g in range(2):
            weigh(7, g)
        quantize_windows(6, 7)
        multiply_early(3, 4)

        take_x(2, (SCALAR, SCALAR), (6, 7))
        stage_x_pass(2, 0, VECTOR)
        take_x(3, (VECTOR, SCALAR), (3, 1))
        quantize_x(2, 0, 1, over="x3")
        stage_x_pass(2, 1, SCALAR, over="x3", at=2 * PASS)
        quantize_x(2, 1, 2)

        def multiply_late(j, banks):
            for h in range(2):
                bank_tile("x%d_half%d" % (j, h), banks[h])
            for g in range(2):
                for h in range(2):
                    multiply(j, PASS * h, PASS * (h + 1), g, "x%d_half%d" % (j, h))

        multiply_late(2, (6, 7))
        put_quarter(2, VECTOR, over="x3", at=2 * BANK_BYTES)
        for g in range(2):
            stage_x_pass(3, g, SCALAR)
            quantize_x(3, g, g + 1)
        put_quarter(3, SCALAR, over="x_listed31")
        multiply_late(3, (5, 2))
        for h in range(2):
            put_out("x2_half%d" % h, 0, PASS, [2], PASS * h, (VECTOR, SCALAR)[h])
        for c0 in (0, QUARTER):
            for h in range(2):
                put_out("x3_half%d" % h, c0, c0 + QUARTER, [3], PASS * h + c0, (VECTOR, SCALAR)[h])
